import numpy as np
import ml_dtypes


def mxq(x, axis, fmt="e4m3"):
    dtype, down = {"e4m3": (ml_dtypes.float8_e4m3fn, 7), "e5m2": (ml_dtypes.float8_e5m2, 14)}[fmt]
    v = np.moveaxis(np.asarray(x, np.float32).astype(ml_dtypes.bfloat16).astype(np.float64), axis, -1)
    blocks = v.reshape(v.shape[:-1] + (-1, 32))
    amax = np.abs(blocks).max(-1, keepdims=True)
    byte = np.maximum(np.where(amax > 0, np.frexp(amax)[1] - 1 + 127, 0) - down, 1)
    scale = np.exp2(byte - 127.0)
    codes = (blocks / scale).astype(np.float32).astype(dtype).astype(np.float64)
    return np.moveaxis((codes * scale).reshape(v.shape), -1, axis)


WIDE = False


def mx_kscale(k):
    if not WIDE:
        return np.ones(k)
    levels = np.array([18, -18])
    if k % 512:
        return np.exp2(np.random.permutation(np.resize(levels, k // 32))).repeat(32)
    a = np.empty((k // 512, 16))
    for p in range(k // 512):
        a[p, :8] = np.random.permutation(np.resize(levels, 8))
        for g in range(8):
            far = levels[np.abs(levels - a[p, g]) >= 10]
            a[p, g + 8] = far[np.random.randint(len(far))]
    return np.exp2(a.ravel()).repeat(32)


def f64(x):
    return np.asarray(x).astype(np.float64)


def striped(idx):
    return np.tile(np.asarray(idx).reshape(-1, 16).T, (8, 1)).astype(np.uint16)


def unstriped(offs):
    return offs[:16].T.reshape(-1).astype(np.int64)


B, N, T, D, DV, R = 1, 512, 2048, 512, 512, 512
PAGE = 32


def setup_inputs():
    n = np.random.standard_normal
    pages = np.random.permutation(T // PAGE)[:B * N // PAGE]
    idx = (pages[:, None] * PAGE + np.arange(PAGE)[None, :]).reshape(-1)
    s = mx_kscale(D)[:, None]
    z = mx_kscale(R)[:, None]
    v = mx_kscale(DV)[:, None]
    q = n((B, D, R))
    do = n((B, DV, R))
    return {
        "qT": (q * s).astype(np.float32),
        "kT": (n((D, T)) * (1.00 / np.sqrt(D)) / s).astype(np.float32),
        "vT": (n((DV, T)) / np.sqrt(DV) / v).astype(np.float32),
        "doT": (do * v).astype(np.float32),
        "rw": (np.random.uniform(0.5, 1.5, (B, R, 1)) * 1.0 / np.sqrt(R) * z).astype(np.float32),
        "qm": (q.transpose(0, 2, 1) / z).astype(np.float32),
        "dom": (do.transpose(0, 2, 1) / z).astype(np.float32),
        "offs": striped(idx),
    }


def reference(qT, kT, vT, doT, rw, qm, dom, offs):
    idx = unstriped(offs)
    pick = lambda x: x[:, idx].reshape(x.shape[0], B, N).transpose(1, 0, 2)
    a = mxq(f64(qT), 1, "e4m3").transpose(0, 2, 1) @ mxq(pick(f64(kT)), 1, "e4m3")
    p = np.square(np.maximum(a, 0.0))
    dp = mxq(f64(doT), 1, "e5m2").transpose(0, 2, 1) @ mxq(pick(f64(vT)), 1, "e4m3")
    ds = f64(rw) * dp * 2.0 * np.maximum(a, 0.0)
    dk = mxq(f64(qm), 1, "e4m3").transpose(0, 2, 1) @ mxq(ds, 1, "e5m2")
    dv = mxq(f64(dom), 1, "e5m2").transpose(0, 2, 1) @ mxq(f64(rw) * p, 1, "e4m3")
    gk = np.zeros((D, T))
    gk[:, idx] = dk.transpose(1, 0, 2).reshape(D, B * N)
    gv = np.zeros((DV, T))
    gv[:, idx] = dv.transpose(1, 0, 2).reshape(DV, B * N)
    return gk, gv

@@ -1,0 +1,173 @@
+from contextlib import ExitStack
+
+import concourse.mybir as mybir
+
+N, T, D, DV, R = 512, 2048, 512, 512, 512
+FLOPS = 4 * 2 * 512 * 512 * 512
+
+F32 = mybir.dt.float32
+BF16 = mybir.dt.bfloat16
+U32 = mybir.dt.uint32
+U16 = mybir.dt.uint16
+U8 = mybir.dt.uint8
+E4M3 = mybir.dt.float8_e4m3fn_x4
+E5M2 = mybir.dt.float8_e5m2_x4
+MULT = mybir.AluOpType.mult
+ACT = mybir.ActivationFunctionType
+
+P = 128
+PACK = 4
+W = 512
+HALF = W // 2
+
+
+def tile_attend_gat_kv_kernel(tc, qT, kT, vT, doT, rw, qm, dom, offs, out_0, out_1):
+    nc = tc.nc
+    with ExitStack() as ctx:
+        keep = ctx.enter_context(tc.tile_pool(name="keep", bufs=1))
+        ring = ctx.enter_context(tc.tile_pool(name="ring", bufs=2))
+        stage = ctx.enter_context(tc.tile_pool(name="stage", bufs=4))
+        psum = ctx.enter_context(tc.psum_pool(name="psum", bufs=1))
+
+        def load_rows(name, src):
+            raw = keep.tile([P, PACK, W], F32, name=name)
+            nc.sync.dma_start(out=raw[:], in_=src.rearrange("(p j) w -> p j w", j=PACK))
+            return raw
+
+        def load_plane(name, pool_hbm, j):
+            plane = keep.tile([P, T], F32, name=name)
+            nc.sync.dma_start(out=plane[:], in_=pool_hbm.rearrange("(p j) w -> p j w", j=PACK)[:, j, :])
+            return plane
+
+        def operand(name):
+            grouped = keep.tile([P, W, PACK], BF16, name=name + "_grouped", align_bytes=64)
+            codes = keep.tile([P, W], U32, name=name + "_codes", align_bytes=64)
+            scales = keep.tile([P, W], U8, name=name + "_scales", align_bytes=64)
+            return grouped, codes, scales
+
+        def interleave(copy, op, rows, lo, hi, run):
+            copy(
+                out=op[0][:, lo:hi, :].rearrange("p (c i) j -> p c j i", i=run),
+                in_=rows[:, :, lo:hi].rearrange("p j (c i) -> p c j i", i=run),
+            )
+
+        def interleave_sorted(copy, op, rows, half):
+            copy(
+                out=op[0][:, half * HALF : (half + 1) * HALF, :].rearrange("p (t m) j -> p m j t", t=2),
+                in_=rows[:].rearrange("p j (m t) -> p m j t", t=PACK)[:, :, :, 2 * half : 2 * half + 2],
+            )
+
+        def quantize(op, fmt, lo, hi):
+            nc.vector.quantize_mx(
+                out=op[1][:, lo:hi].bitcast(fmt),
+                scales=op[2][:, lo:hi],
+                in_=op[0][:, lo:hi, :].rearrange("p w j -> p (w j)"),
+            )
+
+        def matmul(out, lhs, lhs_fmt, m0, rhs, rhs_fmt, lo, hi):
+            nc.tensor.matmul_mx(
+                out=out,
+                lhsT=lhs[1][:, m0 : m0 + P].bitcast(lhs_fmt),
+                lhsT_scale=lhs[2][:, m0 : m0 + P],
+                rhs=rhs[1][:, lo:hi].bitcast(rhs_fmt),
+                rhs_scale=rhs[2][:, lo:hi],
+                start=True,
+                stop=True,
+            )
+
+        vcopy = nc.vector.tensor_copy
+        scopy = nc.scalar.copy
+
+        q_raw = load_rows("q_raw", qT[0])
+        offsets = keep.tile([P, N // 16], U16, name="offsets")
+        nc.sync.dma_start(offsets[:], offs)
+        gate = keep.tile([P, PACK], F32, name="gate")
+        nc.sync.dma_start(out=gate[:], in_=rw[0].rearrange("(p t) o -> p (t o)", t=PACK))
+        k_planes = [load_plane("k_plane%d" % j, kT, j) for j in range(PACK)]
+        dom_raw = load_rows("dom_raw", dom[0])
+        v_planes = [load_plane("v_plane%d" % j, vT, j) for j in range(PACK - 1)]
+        do_raw = load_rows("do_raw", doT[0])
+        v_planes.append(load_plane("v_plane3", vT, 3))
+        qm_raw = load_rows("qm_raw", qm[0])
+
+        q_op, k_op, pw_op, dom_op = operand("q"), operand("k"), operand("pw"), operand("dom")
+        do_op, v_op, ds_op, qm_op = operand("do"), operand("v"), operand("ds"), operand("qm")
+
+        def gather(rows, planes, j):
+            nc.vector.tensor_copy(rows[:, j, :], planes[j][:].indirect(offsets[:]))
+
+        for half in range(2):
+            interleave_sorted(scopy, q_op, q_raw, half)
+        quantize(q_op, E4M3, 0, W)
+        k_rows = keep.tile([P, PACK, W], F32, name="k_rows", tag="gathered")
+        for j in range(PACK):
+            gather(k_rows, k_planes, j)
+        windows = [keep.tile([P, T], F32, name="window%d" % b) for b in range(PACK)]
+        for b in range(PACK):
+            nc.vector.memset(windows[b][:], 0.0)
+        interleave(vcopy, k_op, k_rows, 0, W, 2)
+        quantize(k_op, E4M3, 0, W)
+        interleave(vcopy, dom_op, dom_raw, 0, W, 2)
+        quantize(dom_op, E5M2, 0, W)
+
+        relu2a = keep.tile([P, PACK, W], F32, name="relu2a")
+        v_rows = keep.tile([P, PACK, W], F32, name="v_rows", tag="gathered")
+        gate_rows = gate[:].unsqueeze(1).to_broadcast([P, P, PACK])
+        for c in range(PACK):
+            lo, hi = c * P, (c + 1) * P
+            bank = psum.tile([P, PACK, P], F32, name="score%d" % c, tag="first%d" % c)
+            for t in range(PACK):
+                matmul(bank[:, t, :], q_op, E4M3, t * P, k_op, E4M3, lo, hi)
+            nc.scalar.activation(relu2a[:, :, lo:hi], bank[:], ACT.Relu, scale=2.0)
+            p_rows = ring.tile([P, P, PACK], F32, name="p_rows")
+            nc.scalar.activation(
+                p_rows[:].rearrange("p (c i) t -> p c t i", i=2),
+                relu2a[:, :, lo:hi].rearrange("p t (c i) -> p c t i", i=2),
+                ACT.Square,
+                scale=0.5,
+            )
+            nc.vector.tensor_tensor(pw_op[0][:, lo:hi, :], p_rows[:], gate_rows, MULT)
+            if c > 0:
+                quantize(pw_op, E4M3, lo - P, lo)
+            if c < 2:
+                gather(v_rows, v_planes, c)
+        quantize(pw_op, E4M3, W - P, W)
+        gather(v_rows, v_planes, 2)
+
+        def product(name, lhs, lhs_fmt, rhs, rhs_fmt, b):
+            bank = psum.tile([P, W], F32, name=name + "_bank", tag="second%d" % b)
+            matmul(bank[:], lhs, lhs_fmt, b * P, rhs, rhs_fmt, 0, W)
+            dense = stage.tile([P, W], F32, name="dense")
+            nc.scalar.copy(out=dense[:], in_=bank[:])
+            return dense
+
+        def scatter_store(dense, out, b):
+            nc.vector.tensor_copy(windows[b][:].indirect(offsets[:]), dense[:])
+            nc.sync.dma_start(out=out[b * P : (b + 1) * P, :], in_=windows[b][:])
+
+        dv = [product("dv%d" % b, dom_op, E5M2, pw_op, E4M3, b) for b in range(PACK)]
+        for half in range(2):
+            interleave_sorted(scopy, do_op, do_raw, half)
+        for b in range(3):
+            scatter_store(dv[b], out_1, b)
+        gather(v_rows, v_planes, 3)
+        interleave(vcopy, v_op, v_rows, 0, HALF, 2)
+        interleave(scopy, v_op, v_rows, HALF, W, 2)
+        quantize(do_op, E5M2, 0, W)
+        quantize(v_op, E4M3, 0, W)
+        scatter_store(dv[3], out_1, 3)
+        interleave(scopy, qm_op, qm_raw, 0, W, 2)
+
+        ds_rows = keep.tile([P, PACK, W], BF16, name="ds_rows")
+        for t in range(PACK):
+            bank = psum.tile([P, W], F32, name="dp%d" % t, tag="first%d" % t)
+            matmul(bank[:], do_op, E5M2, t * P, v_op, E4M3, 0, W)
+            nc.vector.scalar_tensor_tensor(ds_rows[:, t, :], bank[:], gate[:, t : t + 1], relu2a[:, t, :], MULT, MULT)
+        interleave(vcopy, ds_op, ds_rows, 0, HALF, 4)
+        interleave(scopy, ds_op, ds_rows, HALF, W, 4)
+        quantize(qm_op, E4M3, 0, W)
+        quantize(ds_op, E5M2, 0, HALF)
+        quantize(ds_op, E5M2, HALF, W)
+        dk = [product("dk%d" % b, qm_op, E4M3, ds_op, E5M2, b) for b in range(PACK)]
+        for b in range(PACK):
+            scatter_store(dk[b], out_0, b)

@@ -19,19 +19,20 @@ P = 128
 PACK = 4
 W = 512
 HALF = W // 2
+WINDOWS = 3
 
 
 def tile_attend_gat_kv_kernel(tc, qT, kT, vT, doT, rw, qm, dom, offs, out_0, out_1):
     nc = tc.nc
     with ExitStack() as ctx:
         keep = ctx.enter_context(tc.tile_pool(name="keep", bufs=1))
-        ring = ctx.enter_context(tc.tile_pool(name="ring", bufs=2))
+        ring = ctx.enter_context(tc.tile_pool(name="ring", bufs=4))
         stage = ctx.enter_context(tc.tile_pool(name="stage", bufs=4))
         psum = ctx.enter_context(tc.psum_pool(name="psum", bufs=1))
 
-        def load_rows(name, src):
-            raw = keep.tile([P, PACK, W], F32, name=name)
-            nc.sync.dma_start(out=raw[:], in_=src.rearrange("(p j) w -> p j w", j=PACK))
+        def load_rows(name, src, lo, hi):
+            raw = keep.tile([P, PACK, hi - lo], F32, name=name)
+            nc.sync.dma_start(out=raw[:], in_=src.rearrange("(p j) w -> p j w", j=PACK)[:, :, lo:hi])
             return raw
 
         def load_plane(name, pool_hbm, j):
@@ -45,10 +46,10 @@ def tile_attend_gat_kv_kernel(tc, qT, kT, vT, doT, rw, qm, dom, offs, out_0, out
             scales = keep.tile([P, W], U8, name=name + "_scales", align_bytes=64)
             return grouped, codes, scales
 
-        def interleave(copy, op, rows, lo, hi, run):
+        def interleave(copy, op, rows, lo, hi, run, first=0):
             copy(
                 out=op[0][:, lo:hi, :].rearrange("p (c i) j -> p c j i", i=run),
-                in_=rows[:, :, lo:hi].rearrange("p j (c i) -> p c j i", i=run),
+                in_=rows[:, :, lo - first : hi - first].rearrange("p j (c i) -> p c j i", i=run),
             )
 
         def interleave_sorted(copy, op, rows, half):
@@ -78,96 +79,160 @@ def tile_attend_gat_kv_kernel(tc, qT, kT, vT, doT, rw, qm, dom, offs, out_0, out
         vcopy = nc.vector.tensor_copy
         scopy = nc.scalar.copy
 
-        q_raw = load_rows("q_raw", qT[0])
+        k_planes, v_planes = {}, {}
         offsets = keep.tile([P, N // 16], U16, name="offsets")
-        nc.sync.dma_start(offsets[:], offs)
         gate = keep.tile([P, PACK], F32, name="gate")
-        nc.sync.dma_start(out=gate[:], in_=rw[0].rearrange("(p t) o -> p (t o)", t=PACK))
-        k_planes = [load_plane("k_plane%d" % j, kT, j) for j in range(PACK)]
-        dom_raw = load_rows("dom_raw", dom[0])
-        v_planes = [load_plane("v_plane%d" % j, vT, j) for j in range(PACK - 1)]
-        do_raw = load_rows("do_raw", doT[0])
-        v_planes.append(load_plane("v_plane3", vT, 3))
-        qm_raw = load_rows("qm_raw", qm[0])
 
         q_op, k_op, pw_op, dom_op = operand("q"), operand("k"), operand("pw"), operand("dom")
         do_op, v_op, ds_op, qm_op = operand("do"), operand("v"), operand("ds"), operand("qm")
-
-        def gather(rows, planes, j):
-            nc.vector.tensor_copy(rows[:, j, :], planes[j][:].indirect(offsets[:]))
-
-        for half in range(2):
-            interleave_sorted(scopy, q_op, q_raw, half)
-        quantize(q_op, E4M3, 0, W)
-        k_rows = keep.tile([P, PACK, W], F32, name="k_rows", tag="gathered")
-        for j in range(PACK):
-            gather(k_rows, k_planes, j)
-        windows = [keep.tile([P, T], F32, name="window%d" % b) for b in range(PACK)]
-        for b in range(PACK):
-            nc.vector.memset(windows[b][:], 0.0)
-        interleave(vcopy, k_op, k_rows, 0, W, 2)
-        quantize(k_op, E4M3, 0, W)
-        interleave(vcopy, dom_op, dom_raw, 0, W, 2)
-        quantize(dom_op, E5M2, 0, W)
-
+        windows = [keep.tile([P, T], F32, name="window%d" % b) for b in range(WINDOWS)]
+        k_rows = keep.tile([P, PACK, W], F32, name="k_rows")
+        v_rows = keep.tile([P, PACK, W], F32, name="v_rows")
         relu2a = keep.tile([P, PACK, W], F32, name="relu2a")
-        v_rows = keep.tile([P, PACK, W], F32, name="v_rows", tag="gathered")
+        ds_rows = keep.tile([P, PACK, W], BF16, name="ds_rows")
         gate_rows = gate[:].unsqueeze(1).to_broadcast([P, P, PACK])
-        for c in range(PACK):
-            lo, hi = c * P, (c + 1) * P
+        p_rows = {}
+        dense = {}
+
+        def zero_windows():
+            for window in windows:
+                nc.vector.memset(window[:], 0.0)
+
+        def gather(rows, planes, j, lo=0, hi=W):
+            nc.vector.tensor_copy(rows[:, j, lo:hi], planes[j][:].indirect(offsets[:, lo // 16 : hi // 16]))
+
+        def scores(c):
             bank = psum.tile([P, PACK, P], F32, name="score%d" % c, tag="first%d" % c)
             for t in range(PACK):
-                matmul(bank[:, t, :], q_op, E4M3, t * P, k_op, E4M3, lo, hi)
-            nc.scalar.activation(relu2a[:, :, lo:hi], bank[:], ACT.Relu, scale=2.0)
-            p_rows = ring.tile([P, P, PACK], F32, name="p_rows")
+                matmul(bank[:, t, :], q_op, E4M3, t * P, k_op, E4M3, c * P, (c + 1) * P)
+            nc.scalar.activation(relu2a[:, :, c * P : (c + 1) * P], bank[:], ACT.Relu, scale=2.0)
+
+        def square_scalar(c):
+            p_rows[c] = ring.tile([P, P, PACK], F32, name="p_rows%d" % c, tag="p_rows")
             nc.scalar.activation(
-                p_rows[:].rearrange("p (c i) t -> p c t i", i=2),
-                relu2a[:, :, lo:hi].rearrange("p t (c i) -> p c t i", i=2),
+                p_rows[c][:].rearrange("p (c i) t -> p c t i", i=2),
+                relu2a[:, :, c * P : (c + 1) * P].rearrange("p t (c i) -> p c t i", i=2),
                 ACT.Square,
                 scale=0.5,
             )
-            nc.vector.tensor_tensor(pw_op[0][:, lo:hi, :], p_rows[:], gate_rows, MULT)
-            if c > 0:
-                quantize(pw_op, E4M3, lo - P, lo)
-            if c < 2:
-                gather(v_rows, v_planes, c)
-        quantize(pw_op, E4M3, W - P, W)
-        gather(v_rows, v_planes, 2)
 
-        def product(name, lhs, lhs_fmt, rhs, rhs_fmt, b):
-            bank = psum.tile([P, W], F32, name=name + "_bank", tag="second%d" % b)
+        def square_vector(c):
+            p_rows[c] = ring.tile([P, P, PACK], F32, name="p_rows%d" % c, tag="p_rows")
+            rows = relu2a[:, :, c * P : (c + 1) * P].rearrange("p t i -> p i t")
+            nc.vector.scalar_tensor_tensor(p_rows[c][:], rows, 0.25, rows, MULT, MULT)
+
+        def weights(c):
+            nc.vector.tensor_tensor(pw_op[0][:, c * P : (c + 1) * P, :], p_rows[c][:], gate_rows, MULT)
+
+        def product(n, copy=scopy):
+            lhs, lhs_fmt, rhs, rhs_fmt = (dom_op, E5M2, pw_op, E4M3) if n < PACK else (qm_op, E4M3, ds_op, E5M2)
+            b = n % PACK
+            bank = psum.tile([P, W], F32, name="product%d" % n, tag="second%d" % b)
             matmul(bank[:], lhs, lhs_fmt, b * P, rhs, rhs_fmt, 0, W)
-            dense = stage.tile([P, W], F32, name="dense")
-            nc.scalar.copy(out=dense[:], in_=bank[:])
-            return dense
+            dense[n] = stage.tile([P, W], F32, name="dense%d" % n, tag="dense")
+            copy(out=dense[n][:], in_=bank[:])
 
-        def scatter_store(dense, out, b):
-            nc.vector.tensor_copy(windows[b][:].indirect(offsets[:]), dense[:])
-            nc.sync.dma_start(out=out[b * P : (b + 1) * P, :], in_=windows[b][:])
+        def scatter_store(n):
+            window, out, b = windows[n % WINDOWS], out_1 if n < PACK else out_0, n % PACK
+            nc.vector.tensor_copy(window[:].indirect(offsets[:]), dense[n][:])
+            nc.sync.dma_start(out=out[b * P : (b + 1) * P, :], in_=window[:])
 
-        dv = [product("dv%d" % b, dom_op, E5M2, pw_op, E4M3, b) for b in range(PACK)]
-        for half in range(2):
-            interleave_sorted(scopy, do_op, do_raw, half)
-        for b in range(3):
-            scatter_store(dv[b], out_1, b)
-        gather(v_rows, v_planes, 3)
-        interleave(vcopy, v_op, v_rows, 0, HALF, 2)
-        interleave(scopy, v_op, v_rows, HALF, W, 2)
-        quantize(do_op, E5M2, 0, W)
-        quantize(v_op, E4M3, 0, W)
-        scatter_store(dv[3], out_1, 3)
-        interleave(scopy, qm_op, qm_raw, 0, W, 2)
-
-        ds_rows = keep.tile([P, PACK, W], BF16, name="ds_rows")
-        for t in range(PACK):
+        def score_gradient(t):
             bank = psum.tile([P, W], F32, name="dp%d" % t, tag="first%d" % t)
             matmul(bank[:], do_op, E5M2, t * P, v_op, E4M3, 0, W)
             nc.vector.scalar_tensor_tensor(ds_rows[:, t, :], bank[:], gate[:, t : t + 1], relu2a[:, t, :], MULT, MULT)
-        interleave(vcopy, ds_op, ds_rows, 0, HALF, 4)
-        interleave(scopy, ds_op, ds_rows, HALF, W, 4)
-        quantize(qm_op, E4M3, 0, W)
-        quantize(ds_op, E5M2, 0, HALF)
+
+        q_raw = load_rows("q_raw", qT[0], 0, W)
+        nc.sync.dma_start(offsets[:], offs)
+        k_planes[0] = load_plane("k_plane0", kT, 0)
+        k_planes[1] = load_plane("k_plane1", kT, 1)
+        k_planes[2] = load_plane("k_plane2", kT, 2)
+        k_planes[3] = load_plane("k_plane3", kT, 3)
+        nc.sync.dma_start(out=gate[:], in_=rw[0].rearrange("(p t) o -> p (t o)", t=PACK))
+        v_planes[0] = load_plane("v_plane0", vT, 0)
+        v_planes[1] = load_plane("v_plane1", vT, 1)
+        v_planes[2] = load_plane("v_plane2", vT, 2)
+        dom_lo = load_rows("dom_lo", dom[0], 0, HALF)
+        v_planes[3] = load_plane("v_plane3", vT, 3)
+        do_raw = load_rows("do_raw", doT[0], 0, W)
+        dom_hi = load_rows("dom_hi", dom[0], HALF, W)
+        qm_hi = load_rows("qm_hi", qm[0], HALF, W)
+        interleave_sorted(vcopy, q_op, q_raw, 0)
+        interleave_sorted(scopy, q_op, q_raw, 1)
+        quantize(q_op, E4M3, 0, W)
+        gather(k_rows, k_planes, 0)
+        qm_lo = load_rows("qm_lo", qm[0], 0, HALF)
+        gather(k_rows, k_planes, 1)
+        gather(k_rows, k_planes, 2)
+        zero_windows()
+        gather(k_rows, k_planes, 3, 0, HALF)
+        gather(k_rows, k_planes, 3, HALF, W)
+        interleave(vcopy, k_op, k_rows, 0, HALF, 2)
+        interleave(scopy, k_op, k_rows, HALF, W, 2)
+        quantize(k_op, E4M3, 0, HALF)
+        quantize(k_op, E4M3, HALF, W)
+        gather(v_rows, v_planes, 0)
+        scores(0)
+        scores(1)
+        square_vector(0)
+        square_scalar(1)
+        scores(2)
+        scores(3)
+        square_scalar(2)
+        square_scalar(3)
+        weights(0)
+        weights(1)
+        gather(v_rows, v_planes, 1)
+        quantize(pw_op, E4M3, 0, HALF)
+        weights(2)
+        weights(3)
+        gather(v_rows, v_planes, 2)
+        quantize(pw_op, E4M3, HALF, HALF + P)
+        quantize(pw_op, E4M3, HALF + P, W)
+        interleave(scopy, dom_op, dom_lo, 0, HALF, 2)
+        quantize(dom_op, E5M2, 0, HALF)
+        product(0, scopy)
+        product(1, scopy)
+        gather(v_rows, v_planes, 3)
+        interleave(vcopy, v_op, v_rows, 0, HALF, 2)
+        interleave(vcopy, v_op, v_rows, HALF, W, 2)
+        scatter_store(0)
+        quantize(v_op, E4M3, 0, HALF)
+        quantize(v_op, E4M3, HALF, W)
+        interleave_sorted(scopy, do_op, do_raw, 0)
+        interleave_sorted(scopy, do_op, do_raw, 1)
+        scatter_store(1)
+        quantize(do_op, E5M2, 0, HALF)
+        interleave(vcopy, dom_op, dom_hi, HALF, HALF + P, 2, HALF)
+        interleave(vcopy, dom_op, dom_hi, HALF + P, W, 2, HALF)
+        quantize(do_op, E5M2, HALF, W)
+        quantize(dom_op, E5M2, HALF, HALF + P)
+        product(2, scopy)
+        score_gradient(0)
+        score_gradient(1)
+        quantize(dom_op, E5M2, HALF + P, W)
+        score_gradient(2)
+        score_gradient(3)
+        product(3, scopy)
+        interleave(scopy, qm_op, qm_lo, 0, P, 2)
+        interleave(scopy, qm_op, qm_lo, P, HALF, 2)
+        scatter_store(2)
+        interleave(scopy, ds_op, ds_rows, 0, P, 4)
+        interleave(vcopy, ds_op, ds_rows, HALF, HALF + P, 4)
+        interleave(vcopy, ds_op, ds_rows, HALF + P, W, 4)
+        interleave(vcopy, ds_op, ds_rows, P, HALF, 4)
+        quantize(qm_op, E4M3, 0, P)
         quantize(ds_op, E5M2, HALF, W)
-        dk = [product("dk%d" % b, qm_op, E4M3, ds_op, E5M2, b) for b in range(PACK)]
-        for b in range(PACK):
-            scatter_store(dk[b], out_0, b)
+        quantize(ds_op, E5M2, 0, HALF)
+        scatter_store(3)
+        quantize(qm_op, E4M3, P, HALF)
+        interleave(scopy, qm_op, qm_hi, HALF, W, 2, HALF)
+        quantize(qm_op, E4M3, HALF, W)
+        product(4, scopy)
+        scatter_store(4)
+        product(5, scopy)
+        scatter_store(5)
+        product(6, scopy)
+        scatter_store(6)
+        product(7, scopy)
+        scatter_store(7)

@@ -2,8 +2,9 @@ from contextlib import ExitStack
 
 import concourse.mybir as mybir
 
-N, T, D, DV, R = 512, 2048, 512, 512, 512
-FLOPS = 4 * 2 * 512 * 512 * 512
+TOKENS = 2048
+W = 512
+FLOPS = 4 * 2 * W * W * W
 
 F32 = mybir.dt.float32
 BF16 = mybir.dt.bfloat16
@@ -17,17 +18,19 @@ ACT = mybir.ActivationFunctionType
 
 P = 128
 PACK = 4
-W = 512
 HALF = W // 2
-WINDOWS = 3
+LIST_ROWS = 16
+ALIGN = 64
+WINDOW_OF = (0, 1, 2, 0, 3, 1, 2, 0)
 
 
 def tile_attend_gat_kv_kernel(tc, qT, kT, vT, doT, rw, qm, dom, offs, out_0, out_1):
     nc = tc.nc
+    vcopy = nc.vector.tensor_copy
+    scopy = nc.scalar.copy
     with ExitStack() as ctx:
         keep = ctx.enter_context(tc.tile_pool(name="keep", bufs=1))
-        ring = ctx.enter_context(tc.tile_pool(name="ring", bufs=4))
-        stage = ctx.enter_context(tc.tile_pool(name="stage", bufs=4))
+        stage = ctx.enter_context(tc.tile_pool(name="stage", bufs=PACK))
         psum = ctx.enter_context(tc.psum_pool(name="psum", bufs=1))
 
         def load_rows(name, src, lo, hi):
@@ -36,203 +39,201 @@ def tile_attend_gat_kv_kernel(tc, qT, kT, vT, doT, rw, qm, dom, offs, out_0, out
             return raw
 
         def load_plane(name, pool_hbm, j):
-            plane = keep.tile([P, T], F32, name=name)
+            plane = keep.tile([P, TOKENS], F32, name=name)
             nc.sync.dma_start(out=plane[:], in_=pool_hbm.rearrange("(p j) w -> p j w", j=PACK)[:, j, :])
             return plane
 
-        def operand(name):
-            grouped = keep.tile([P, W, PACK], BF16, name=name + "_grouped", align_bytes=64)
-            codes = keep.tile([P, W], U32, name=name + "_codes", align_bytes=64)
-            scales = keep.tile([P, W], U8, name=name + "_scales", align_bytes=64)
-            return grouped, codes, scales
+        def operand(name, fmt, width=W, tag=None):
+            grouped = keep.tile([P, width, PACK], BF16, name=name + "_grouped", tag=tag or name, align_bytes=ALIGN)
+            codes = keep.tile([P, width], U32, name=name + "_codes", align_bytes=ALIGN)
+            scales = keep.tile([P, width], U8, name=name + "_scales", align_bytes=ALIGN)
+            return grouped, codes, scales, fmt
 
-        def interleave(copy, op, rows, lo, hi, run, first=0):
+        def gather(pairs, plane, j):
+            vcopy(pairs[:, j // 2, :, j % 2], plane[:].indirect(offsets[:]))
+
+        def group_pairs(copy, op, pairs, lo, hi):
             copy(
-                out=op[0][:, lo:hi, :].rearrange("p (c i) j -> p c j i", i=run),
-                in_=rows[:, :, lo - first : hi - first].rearrange("p j (c i) -> p c j i", i=run),
+                out=op[0][:, lo:hi, :].bitcast(F32).rearrange("p (c i) u -> p c u i", i=2),
+                in_=pairs[:, :, lo:hi, :].rearrange("p u w e -> p u (w e)").bitcast(F32).rearrange("p u (c i) -> p c u i", i=2),
             )
 
-        def interleave_sorted(copy, op, rows, half):
+        def group(copy, op, lo, rows, first, count):
+            run = 2 if rows.dtype == F32 else 4
+            copy(
+                out=op[0][:, lo : lo + count, :].rearrange("p (c i) j -> p c j i", i=run),
+                in_=rows[:, :, first : first + count].rearrange("p j (c i) -> p c j i", i=run),
+            )
+
+        def group_sorted(copy, op, rows, half):
             copy(
                 out=op[0][:, half * HALF : (half + 1) * HALF, :].rearrange("p (t m) j -> p m j t", t=2),
                 in_=rows[:].rearrange("p j (m t) -> p m j t", t=PACK)[:, :, :, 2 * half : 2 * half + 2],
             )
 
-        def quantize(op, fmt, lo, hi):
+        def quantize(op, lo, hi):
+            grouped, codes, scales, fmt = op
             nc.vector.quantize_mx(
-                out=op[1][:, lo:hi].bitcast(fmt),
-                scales=op[2][:, lo:hi],
-                in_=op[0][:, lo:hi, :].rearrange("p w j -> p (w j)"),
+                out=codes[:, lo:hi].bitcast(fmt),
+                scales=scales[:, lo:hi],
+                in_=grouped[:, lo:hi, :].rearrange("p w j -> p (w j)"),
             )
 
-        def matmul(out, lhs, lhs_fmt, m0, rhs, rhs_fmt, lo, hi):
+        def matmul(out, lhs, m0, rhs, lo, hi):
             nc.tensor.matmul_mx(
                 out=out,
-                lhsT=lhs[1][:, m0 : m0 + P].bitcast(lhs_fmt),
+                lhsT=lhs[1][:, m0 : m0 + P].bitcast(lhs[3]),
                 lhsT_scale=lhs[2][:, m0 : m0 + P],
-                rhs=rhs[1][:, lo:hi].bitcast(rhs_fmt),
+                rhs=rhs[1][:, lo:hi].bitcast(rhs[3]),
                 rhs_scale=rhs[2][:, lo:hi],
                 start=True,
                 stop=True,
             )
 
-        vcopy = nc.vector.tensor_copy
-        scopy = nc.scalar.copy
-
-        k_planes, v_planes = {}, {}
-        offsets = keep.tile([P, N // 16], U16, name="offsets")
+        offsets = keep.tile([P, W // LIST_ROWS], U16, name="offsets")
         gate = keep.tile([P, PACK], F32, name="gate")
+        k_planes = [load_plane("k_plane0", kT, 0)]
+        nc.sync.dma_start(offsets[:], offs)
+        k_planes.extend(load_plane("k_plane%d" % j, kT, j) for j in range(1, PACK))
+        q_raw = load_rows("q_raw", qT[0], 0, W)
+        v_planes = [load_plane("v_plane%d" % j, vT, j) for j in range(2)]
+        nc.sync.dma_start(out=gate[:], in_=rw[0].rearrange("(p t) o -> p (t o)", t=PACK))
+        v_planes.append(load_plane("v_plane2", vT, 2))
+        dom_lo = load_rows("dom_lo", dom[0], 0, HALF)
+        v_planes.append(load_plane("v_plane3", vT, 3))
+        do_raw = load_rows("do_raw", doT[0], 0, W)
+        dom_hi = load_rows("dom_hi", dom[0], HALF, W)
+        qm_raw = load_rows("qm_raw", qm[0], 0, W)
 
-        q_op, k_op, pw_op, dom_op = operand("q"), operand("k"), operand("pw"), operand("dom")
-        do_op, v_op, ds_op, qm_op = operand("do"), operand("v"), operand("ds"), operand("qm")
-        windows = [keep.tile([P, T], F32, name="window%d" % b) for b in range(WINDOWS)]
-        k_rows = keep.tile([P, PACK, W], F32, name="k_rows")
-        v_rows = keep.tile([P, PACK, W], F32, name="v_rows")
+        q_op, k_op, pw_op, dom_op = operand("q", E4M3), operand("k", E4M3), operand("pw", E4M3), operand("dom", E5M2)
+        do_op, v_op, ds_op = operand("do", E5M2), operand("v", E4M3), operand("ds", E5M2)
+        qm_lo_op = operand("qm_lo", E4M3, HALF)
+        windows = [keep.tile([P, TOKENS], F32, name="window%d" % n) for n in range(max(WINDOW_OF) + 1)]
+        k_pairs = keep.tile([P, 2, W, 2], BF16, name="k_pairs")
+        v_pairs = keep.tile([P, 2, W, 2], BF16, name="v_pairs")
         relu2a = keep.tile([P, PACK, W], F32, name="relu2a")
-        ds_rows = keep.tile([P, PACK, W], BF16, name="ds_rows")
+        ds_rows = keep.tile([P, PACK, W], BF16, name="ds_rows", tag="late", align_bytes=ALIGN)
+        qm_hi_op = operand("qm_hi", E4M3, HALF, "late")
         gate_rows = gate[:].unsqueeze(1).to_broadcast([P, P, PACK])
-        p_rows = {}
-        dense = {}
-
-        def zero_windows():
-            for window in windows:
-                nc.vector.memset(window[:], 0.0)
-
-        def gather(rows, planes, j, lo=0, hi=W):
-            nc.vector.tensor_copy(rows[:, j, lo:hi], planes[j][:].indirect(offsets[:, lo // 16 : hi // 16]))
+        score_banks, squares, dense = {}, {}, {}
 
         def scores(c):
-            bank = psum.tile([P, PACK, P], F32, name="score%d" % c, tag="first%d" % c)
+            score_banks[c] = psum.tile([P, PACK, P], F32, name="score%d" % c, tag="first%d" % c)
             for t in range(PACK):
-                matmul(bank[:, t, :], q_op, E4M3, t * P, k_op, E4M3, c * P, (c + 1) * P)
-            nc.scalar.activation(relu2a[:, :, c * P : (c + 1) * P], bank[:], ACT.Relu, scale=2.0)
+                matmul(score_banks[c][:, t, :], q_op, t * P, k_op, c * P, (c + 1) * P)
+
+        def relu(c):
+            nc.scalar.activation(relu2a[:, :, c * P : (c + 1) * P], score_banks[c][:], ACT.Relu, scale=2.0)
 
         def square_scalar(c):
-            p_rows[c] = ring.tile([P, P, PACK], F32, name="p_rows%d" % c, tag="p_rows")
+            squares[c] = stage.tile([P, P, PACK], F32, name="square%d" % c, tag="square")
             nc.scalar.activation(
-                p_rows[c][:].rearrange("p (c i) t -> p c t i", i=2),
+                squares[c][:].rearrange("p (c i) t -> p c t i", i=2),
                 relu2a[:, :, c * P : (c + 1) * P].rearrange("p t (c i) -> p c t i", i=2),
                 ACT.Square,
                 scale=0.5,
             )
 
         def square_vector(c):
-            p_rows[c] = ring.tile([P, P, PACK], F32, name="p_rows%d" % c, tag="p_rows")
+            squares[c] = stage.tile([P, P, PACK], F32, name="square%d" % c, tag="square")
             rows = relu2a[:, :, c * P : (c + 1) * P].rearrange("p t i -> p i t")
-            nc.vector.scalar_tensor_tensor(p_rows[c][:], rows, 0.25, rows, MULT, MULT)
+            nc.vector.scalar_tensor_tensor(squares[c][:], rows, 0.25, rows, MULT, MULT)
 
         def weights(c):
-            nc.vector.tensor_tensor(pw_op[0][:, c * P : (c + 1) * P, :], p_rows[c][:], gate_rows, MULT)
-
-        def product(n, copy=scopy):
-            lhs, lhs_fmt, rhs, rhs_fmt = (dom_op, E5M2, pw_op, E4M3) if n < PACK else (qm_op, E4M3, ds_op, E5M2)
-            b = n % PACK
-            bank = psum.tile([P, W], F32, name="product%d" % n, tag="second%d" % b)
-            matmul(bank[:], lhs, lhs_fmt, b * P, rhs, rhs_fmt, 0, W)
-            dense[n] = stage.tile([P, W], F32, name="dense%d" % n, tag="dense")
-            copy(out=dense[n][:], in_=bank[:])
-
-        def scatter_store(n):
-            window, out, b = windows[n % WINDOWS], out_1 if n < PACK else out_0, n % PACK
-            nc.vector.tensor_copy(window[:].indirect(offsets[:]), dense[n][:])
-            nc.sync.dma_start(out=out[b * P : (b + 1) * P, :], in_=window[:])
+            nc.vector.tensor_tensor(pw_op[0][:, c * P : (c + 1) * P, :], squares[c][:], gate_rows, MULT)
 
         def score_gradient(t):
             bank = psum.tile([P, W], F32, name="dp%d" % t, tag="first%d" % t)
-            matmul(bank[:], do_op, E5M2, t * P, v_op, E4M3, 0, W)
+            matmul(bank[:], do_op, t * P, v_op, 0, W)
             nc.vector.scalar_tensor_tensor(ds_rows[:, t, :], bank[:], gate[:, t : t + 1], relu2a[:, t, :], MULT, MULT)
 
-        q_raw = load_rows("q_raw", qT[0], 0, W)
-        nc.sync.dma_start(offsets[:], offs)
-        k_planes[0] = load_plane("k_plane0", kT, 0)
-        k_planes[1] = load_plane("k_plane1", kT, 1)
-        k_planes[2] = load_plane("k_plane2", kT, 2)
-        k_planes[3] = load_plane("k_plane3", kT, 3)
-        nc.sync.dma_start(out=gate[:], in_=rw[0].rearrange("(p t) o -> p (t o)", t=PACK))
-        v_planes[0] = load_plane("v_plane0", vT, 0)
-        v_planes[1] = load_plane("v_plane1", vT, 1)
-        v_planes[2] = load_plane("v_plane2", vT, 2)
-        dom_lo = load_rows("dom_lo", dom[0], 0, HALF)
-        v_planes[3] = load_plane("v_plane3", vT, 3)
-        do_raw = load_rows("do_raw", doT[0], 0, W)
-        dom_hi = load_rows("dom_hi", dom[0], HALF, W)
-        qm_hi = load_rows("qm_hi", qm[0], HALF, W)
-        interleave_sorted(vcopy, q_op, q_raw, 0)
-        interleave_sorted(scopy, q_op, q_raw, 1)
-        quantize(q_op, E4M3, 0, W)
-        gather(k_rows, k_planes, 0)
-        qm_lo = load_rows("qm_lo", qm[0], 0, HALF)
-        gather(k_rows, k_planes, 1)
-        gather(k_rows, k_planes, 2)
-        zero_windows()
-        gather(k_rows, k_planes, 3, 0, HALF)
-        gather(k_rows, k_planes, 3, HALF, W)
-        interleave(vcopy, k_op, k_rows, 0, HALF, 2)
-        interleave(scopy, k_op, k_rows, HALF, W, 2)
-        quantize(k_op, E4M3, 0, HALF)
-        quantize(k_op, E4M3, HALF, W)
-        gather(v_rows, v_planes, 0)
-        scores(0)
-        scores(1)
+        def product(n, lhs, m0, rhs):
+            bank = psum.tile([P, W], F32, name="product%d" % n, tag="second%d" % (n % PACK))
+            matmul(bank[:], lhs, m0, rhs, 0, W)
+            dense[n] = stage.tile([P, W], F32, name="dense%d" % n, tag="dense")
+            scopy(out=dense[n][:], in_=bank[:])
+
+        def scatter_store(n):
+            window, out, row = windows[WINDOW_OF[n]], out_1 if n < PACK else out_0, n % PACK * P
+            vcopy(window[:].indirect(offsets[:]), dense[n][:])
+            nc.sync.dma_start(out=out[row : row + P, :], in_=window[:])
+
+
+        for j in range(PACK):
+            gather(k_pairs, k_planes[j], j)
+        for window in windows:
+            nc.vector.memset(window[:], 0.0)
+        group_pairs(vcopy, k_op, k_pairs, 0, HALF)
+        group_pairs(scopy, k_op, k_pairs, HALF, W)
+        quantize(k_op, 0, W)
+        group_sorted(vcopy, q_op, q_raw, 0)
+        group_sorted(scopy, q_op, q_raw, 1)
+        quantize(q_op, 0, HALF)
+        quantize(q_op, HALF, W)
+
+        gather(v_pairs, v_planes[0], 0)
+        for c in range(3):
+            scores(c)
+        for c in range(3):
+            relu(c)
         square_vector(0)
+        gather(v_pairs, v_planes[1], 1)
         square_scalar(1)
-        scores(2)
-        scores(3)
         square_scalar(2)
+        scores(3)
+        relu(3)
         square_scalar(3)
-        weights(0)
-        weights(1)
-        gather(v_rows, v_planes, 1)
-        quantize(pw_op, E4M3, 0, HALF)
-        weights(2)
+        for c in range(3):
+            weights(c)
+        gather(v_pairs, v_planes[2], 2)
+        quantize(pw_op, 2 * P, 3 * P)
         weights(3)
-        gather(v_rows, v_planes, 2)
-        quantize(pw_op, E4M3, HALF, HALF + P)
-        quantize(pw_op, E4M3, HALF + P, W)
-        interleave(scopy, dom_op, dom_lo, 0, HALF, 2)
-        quantize(dom_op, E5M2, 0, HALF)
-        product(0, scopy)
-        product(1, scopy)
-        gather(v_rows, v_planes, 3)
-        interleave(vcopy, v_op, v_rows, 0, HALF, 2)
-        interleave(vcopy, v_op, v_rows, HALF, W, 2)
+        quantize(pw_op, 0, 2 * P)
+        quantize(pw_op, 3 * P, W)
+
+        group(scopy, dom_op, 0, dom_lo, 0, HALF)
+        quantize(dom_op, 0, HALF)
+        product(0, dom_op, 0, pw_op)
+        product(1, dom_op, P, pw_op)
+        gather(v_pairs, v_planes[3], 3)
+        group_pairs(vcopy, v_op, v_pairs, 0, HALF)
+        group_pairs(scopy, v_op, v_pairs, HALF, W)
         scatter_store(0)
-        quantize(v_op, E4M3, 0, HALF)
-        quantize(v_op, E4M3, HALF, W)
-        interleave_sorted(scopy, do_op, do_raw, 0)
-        interleave_sorted(scopy, do_op, do_raw, 1)
         scatter_store(1)
-        quantize(do_op, E5M2, 0, HALF)
-        interleave(vcopy, dom_op, dom_hi, HALF, HALF + P, 2, HALF)
-        interleave(vcopy, dom_op, dom_hi, HALF + P, W, 2, HALF)
-        quantize(do_op, E5M2, HALF, W)
-        quantize(dom_op, E5M2, HALF, HALF + P)
-        product(2, scopy)
-        score_gradient(0)
+        quantize(v_op, 0, W)
+
+        group_sorted(scopy, do_op, do_raw, 0)
+        group_sorted(scopy, do_op, do_raw, 1)
+        group(vcopy, dom_op, 2 * P, dom_hi, 0, P)
+        group(scopy, dom_op, 3 * P, dom_hi, P, P)
+        quantize(do_op, 0, HALF)
+        quantize(dom_op, 2 * P, 3 * P)
         score_gradient(1)
-        quantize(dom_op, E5M2, HALF + P, W)
-        score_gradient(2)
+        quantize(do_op, HALF, W)
+        score_gradient(0)
+        quantize(dom_op, 3 * P, W)
+        group(scopy, qm_lo_op, 0, qm_raw, 0, P)
         score_gradient(3)
-        product(3, scopy)
-        interleave(scopy, qm_op, qm_lo, 0, P, 2)
-        interleave(scopy, qm_op, qm_lo, P, HALF, 2)
+        product(2, dom_op, 2 * P, pw_op)
+        score_gradient(2)
+        group(scopy, qm_lo_op, P, qm_raw, P, P)
+        product(3, dom_op, 3 * P, pw_op)
         scatter_store(2)
-        interleave(scopy, ds_op, ds_rows, 0, P, 4)
-        interleave(vcopy, ds_op, ds_rows, HALF, HALF + P, 4)
-        interleave(vcopy, ds_op, ds_rows, HALF + P, W, 4)
-        interleave(vcopy, ds_op, ds_rows, P, HALF, 4)
-        quantize(qm_op, E4M3, 0, P)
-        quantize(ds_op, E5M2, HALF, W)
-        quantize(ds_op, E5M2, 0, HALF)
+        group(vcopy, ds_op, 0, ds_rows, 0, HALF)
+        group(scopy, ds_op, HALF, ds_rows, HALF, HALF)
+        quantize(qm_lo_op, 0, P)
+        quantize(ds_op, 0, HALF)
+        quantize(ds_op, HALF, W)
         scatter_store(3)
-        quantize(qm_op, E4M3, P, HALF)
-        interleave(scopy, qm_op, qm_hi, HALF, W, 2, HALF)
-        quantize(qm_op, E4M3, HALF, W)
-        product(4, scopy)
+
+        product(4, qm_lo_op, 0, ds_op)
+        quantize(qm_lo_op, P, HALF)
         scatter_store(4)
-        product(5, scopy)
+        product(5, qm_lo_op, P, ds_op)
+        group(scopy, qm_hi_op, 0, qm_raw, HALF, HALF)
+        quantize(qm_hi_op, 0, HALF)
         scatter_store(5)
-        product(6, scopy)
+        product(6, qm_hi_op, 0, ds_op)
         scatter_store(6)
-        product(7, scopy)
+        product(7, qm_hi_op, P, ds_op)
         scatter_store(7)

@@ -21,7 +21,18 @@ PACK = 4
 HALF = W // 2
 LIST_ROWS = 16
 ALIGN = 64
-WINDOW_OF = (0, 1, 2, 0, 3, 1, 2, 0)
+WINDOW_OF = (0, 1, 2, 3, 0, 1, 2, 3)
+LOADS = "k offs gate k k k q v v v dom v do qm"
+GV = 4
+PW_IN = "v_plane0"
+QM2 = None
+QM3 = "ds_rows"
+DENSE_IN = (None, None, "do_raw", "relu_a", None, None, None, None)
+VK = 320
+VQ = 0
+VP = 320
+VV = 192
+VS = 256
 
 
 def tile_attend_gat_kv_kernel(tc, qT, kT, vT, doT, rw, qm, dom, offs, out_0, out_1):
@@ -30,16 +41,15 @@ def tile_attend_gat_kv_kernel(tc, qT, kT, vT, doT, rw, qm, dom, offs, out_0, out
     scopy = nc.scalar.copy
     with ExitStack() as ctx:
         keep = ctx.enter_context(tc.tile_pool(name="keep", bufs=1))
-        stage = ctx.enter_context(tc.tile_pool(name="stage", bufs=PACK))
         psum = ctx.enter_context(tc.psum_pool(name="psum", bufs=1))
 
         def load_rows(name, src, lo, hi):
-            raw = keep.tile([P, PACK, hi - lo], F32, name=name)
+            raw = keep.tile([P, PACK, hi - lo], F32, name=name, align_bytes=ALIGN)
             nc.sync.dma_start(out=raw[:], in_=src.rearrange("(p j) w -> p j w", j=PACK)[:, :, lo:hi])
             return raw
 
         def load_plane(name, pool_hbm, j):
-            plane = keep.tile([P, TOKENS], F32, name=name)
+            plane = keep.tile([P, TOKENS], F32, name=name, align_bytes=ALIGN)
             nc.sync.dma_start(out=plane[:], in_=pool_hbm.rearrange("(p j) w -> p j w", j=PACK)[:, j, :])
             return plane
 
@@ -49,14 +59,8 @@ def tile_attend_gat_kv_kernel(tc, qT, kT, vT, doT, rw, qm, dom, offs, out_0, out
             scales = keep.tile([P, width], U8, name=name + "_scales", align_bytes=ALIGN)
             return grouped, codes, scales, fmt
 
-        def gather(pairs, plane, j):
-            vcopy(pairs[:, j // 2, :, j % 2], plane[:].indirect(offsets[:]))
-
-        def group_pairs(copy, op, pairs, lo, hi):
-            copy(
-                out=op[0][:, lo:hi, :].bitcast(F32).rearrange("p (c i) u -> p c u i", i=2),
-                in_=pairs[:, :, lo:hi, :].rearrange("p u w e -> p u (w e)").bitcast(F32).rearrange("p u (c i) -> p c u i", i=2),
-            )
+        def gather(rows, plane, j, lo=0, hi=W):
+            vcopy(rows[:, j, lo:hi], plane[:].indirect(offsets[:, lo // LIST_ROWS : hi // LIST_ROWS]))
 
         def group(copy, op, lo, rows, first, count):
             run = 2 if rows.dtype == F32 else 4
@@ -92,65 +96,58 @@ def tile_attend_gat_kv_kernel(tc, qT, kT, vT, doT, rw, qm, dom, offs, out_0, out
 
         offsets = keep.tile([P, W // LIST_ROWS], U16, name="offsets")
         gate = keep.tile([P, PACK], F32, name="gate")
-        k_planes = [load_plane("k_plane0", kT, 0)]
-        nc.sync.dma_start(offsets[:], offs)
-        k_planes.extend(load_plane("k_plane%d" % j, kT, j) for j in range(1, PACK))
-        q_raw = load_rows("q_raw", qT[0], 0, W)
-        v_planes = [load_plane("v_plane%d" % j, vT, j) for j in range(2)]
-        nc.sync.dma_start(out=gate[:], in_=rw[0].rearrange("(p t) o -> p (t o)", t=PACK))
-        v_planes.append(load_plane("v_plane2", vT, 2))
-        dom_lo = load_rows("dom_lo", dom[0], 0, HALF)
-        v_planes.append(load_plane("v_plane3", vT, 3))
-        do_raw = load_rows("do_raw", doT[0], 0, W)
-        dom_hi = load_rows("dom_hi", dom[0], HALF, W)
-        qm_raw = load_rows("qm_raw", qm[0], 0, W)
+        raw, k_planes, v_planes = {}, [], []
+        for name in LOADS.split():
+            if name == "offs":
+                nc.sync.dma_start(offsets[:], offs)
+            elif name == "gate":
+                nc.scalar.dma_start(out=gate[:], in_=rw[0].rearrange("(p t) o -> p (t o)", t=PACK))
+            elif name == "k":
+                k_planes.append(load_plane("k_plane%d" % len(k_planes), kT, len(k_planes)))
+            elif name == "v":
+                v_planes.append(load_plane("v_plane%d" % len(v_planes), vT, len(v_planes)))
+            elif name == "q":
+                q_raw = load_rows("q_raw", qT[0], 0, W)
+            elif name == "do":
+                do_raw = load_rows("do_raw", doT[0], 0, W)
+            elif name == "qm":
+                qm_raw = load_rows("qm_raw", qm[0], 0, W)
+            elif name == "dom":
+                dom_raw = load_rows("dom_raw", dom[0], 0, W)
+                dom_lo, dom_hi, hi0 = dom_raw, dom_raw, HALF
+            elif name == "dom_lo":
+                dom_lo = load_rows("dom_lo", dom[0], 0, HALF)
+            elif name == "dom_hi":
+                dom_hi, hi0 = load_rows("dom_hi", dom[0], HALF, W), 0
 
         q_op, k_op, pw_op, dom_op = operand("q", E4M3), operand("k", E4M3), operand("pw", E4M3), operand("dom", E5M2)
-        do_op, v_op, ds_op = operand("do", E5M2), operand("v", E4M3), operand("ds", E5M2)
-        qm_lo_op = operand("qm_lo", E4M3, HALF)
+        do_op, v_op, ds_op, qm_op = operand("do", E5M2), operand("v", E4M3), operand("ds", E5M2), operand("qm", E4M3, P)
         windows = [keep.tile([P, TOKENS], F32, name="window%d" % n) for n in range(max(WINDOW_OF) + 1)]
-        k_pairs = keep.tile([P, 2, W, 2], BF16, name="k_pairs")
-        v_pairs = keep.tile([P, 2, W, 2], BF16, name="v_pairs")
-        relu2a = keep.tile([P, PACK, W], F32, name="relu2a")
-        ds_rows = keep.tile([P, PACK, W], BF16, name="ds_rows", tag="late", align_bytes=ALIGN)
-        qm_hi_op = operand("qm_hi", E4M3, HALF, "late")
-        gate_rows = gate[:].unsqueeze(1).to_broadcast([P, P, PACK])
-        score_banks, squares, dense = {}, {}, {}
+        k_rows = keep.tile([P, PACK, W], BF16, name="k_rows", align_bytes=ALIGN)
+        v_rows = keep.tile([P, PACK, W], BF16, name="v_rows", align_bytes=ALIGN)
+        relu_a = keep.tile([P, PACK, W], F32, name="relu_a", align_bytes=ALIGN)
+        gate2 = keep.tile([P, PACK], F32, name="gate2")
+        ds_rows = keep.tile([P, PACK, W], BF16, name="ds_rows", align_bytes=ALIGN)
+        pw_rows = keep.tile([P, PACK, W], BF16, name="pw_rows", tag=PW_IN or "pw_rows", align_bytes=ALIGN)
+        dense, dp_banks = {}, {}
 
-        def scores(c):
-            score_banks[c] = psum.tile([P, PACK, P], F32, name="score%d" % c, tag="first%d" % c)
-            for t in range(PACK):
-                matmul(score_banks[c][:, t, :], q_op, t * P, k_op, c * P, (c + 1) * P)
-
-        def relu(c):
-            nc.scalar.activation(relu2a[:, :, c * P : (c + 1) * P], score_banks[c][:], ACT.Relu, scale=2.0)
-
-        def square_scalar(c):
-            squares[c] = stage.tile([P, P, PACK], F32, name="square%d" % c, tag="square")
-            nc.scalar.activation(
-                squares[c][:].rearrange("p (c i) t -> p c t i", i=2),
-                relu2a[:, :, c * P : (c + 1) * P].rearrange("p t (c i) -> p c t i", i=2),
-                ACT.Square,
-                scale=0.5,
-            )
-
-        def square_vector(c):
-            squares[c] = stage.tile([P, P, PACK], F32, name="square%d" % c, tag="square")
-            rows = relu2a[:, :, c * P : (c + 1) * P].rearrange("p t i -> p i t")
-            nc.vector.scalar_tensor_tensor(squares[c][:], rows, 0.25, rows, MULT, MULT)
-
-        def weights(c):
-            nc.vector.tensor_tensor(pw_op[0][:, c * P : (c + 1) * P, :], squares[c][:], gate_rows, MULT)
+        def weights(t):
+            bank = psum.tile([P, W], F32, name="score%d" % t, tag="first%d" % t)
+            matmul(bank[:], q_op, t * P, k_op, 0, W)
+            nc.scalar.activation(relu_a[:, t, :], bank[:], ACT.Relu)
+            nc.vector.scalar_tensor_tensor(pw_rows[:, t, :], bank[:], gate[:, t : t + 1], relu_a[:, t, :], MULT, MULT)
 
         def score_gradient(t):
-            bank = psum.tile([P, W], F32, name="dp%d" % t, tag="first%d" % t)
-            matmul(bank[:], do_op, t * P, v_op, 0, W)
-            nc.vector.scalar_tensor_tensor(ds_rows[:, t, :], bank[:], gate[:, t : t + 1], relu2a[:, t, :], MULT, MULT)
+            dp_banks[t] = psum.tile([P, W], F32, name="dp%d" % t, tag="first%d" % t)
+            matmul(dp_banks[t][:], do_op, t * P, v_op, 0, W)
+
+        def ds_part(t, lo, hi):
+            nc.vector.scalar_tensor_tensor(ds_rows[:, t, lo:hi], dp_banks[t][:, lo:hi], gate2[:, t : t + 1], relu_a[:, t, lo:hi], MULT, MULT)
 
         def product(n, lhs, m0, rhs):
             bank = psum.tile([P, W], F32, name="product%d" % n, tag="second%d" % (n % PACK))
             matmul(bank[:], lhs, m0, rhs, 0, W)
-            dense[n] = stage.tile([P, W], F32, name="dense%d" % n, tag="dense")
+            dense[n] = keep.tile([P, W], F32, name="dense%d" % n, tag=DENSE_IN[n] or "dense%d" % (n % PACK), align_bytes=ALIGN)
             scopy(out=dense[n][:], in_=bank[:])
 
         def scatter_store(n):
@@ -158,82 +155,67 @@ def tile_attend_gat_kv_kernel(tc, qT, kT, vT, doT, rw, qm, dom, offs, out_0, out
             vcopy(window[:].indirect(offsets[:]), dense[n][:])
             nc.sync.dma_start(out=out[row : row + P, :], in_=window[:])
 
-
-        for j in range(PACK):
-            gather(k_pairs, k_planes[j], j)
         for window in windows:
             nc.vector.memset(window[:], 0.0)
-        group_pairs(vcopy, k_op, k_pairs, 0, HALF)
-        group_pairs(scopy, k_op, k_pairs, HALF, W)
+        nc.vector.tensor_scalar(gate2[:], gate[:], 2.0, None, MULT)
+        for j in range(PACK):
+            gather(k_rows, k_planes[j], j)
+        group(vcopy, k_op, 0, k_rows, 0, VK)
+        group(scopy, k_op, VK, k_rows, VK, W - VK)
         quantize(k_op, 0, W)
         group_sorted(vcopy, q_op, q_raw, 0)
         group_sorted(scopy, q_op, q_raw, 1)
         quantize(q_op, 0, HALF)
         quantize(q_op, HALF, W)
-
-        gather(v_pairs, v_planes[0], 0)
-        for c in range(3):
-            scores(c)
-        for c in range(3):
-            relu(c)
-        square_vector(0)
-        gather(v_pairs, v_planes[1], 1)
-        square_scalar(1)
-        square_scalar(2)
-        scores(3)
-        relu(3)
-        square_scalar(3)
-        for c in range(3):
-            weights(c)
-        gather(v_pairs, v_planes[2], 2)
-        quantize(pw_op, 2 * P, 3 * P)
-        weights(3)
-        quantize(pw_op, 0, 2 * P)
-        quantize(pw_op, 3 * P, W)
-
+        for j in range(GV):
+            gather(v_rows, v_planes[j], j)
+        for t in range(PACK):
+            weights(t)
+        group(vcopy, pw_op, 0, pw_rows, 0, VP)
+        group(scopy, pw_op, VP, pw_rows, VP, W - VP)
+        quantize(pw_op, 0, HALF)
+        quantize(pw_op, HALF, W)
+        for j in range(GV, PACK):
+            gather(v_rows, v_planes[j], j)
+        group(vcopy, v_op, 0, v_rows, 0, VV)
+        group(scopy, v_op, VV, v_rows, VV, W - VV)
+        quantize(v_op, 0, W)
+        group_sorted(vcopy, do_op, do_raw, 0)
+        group_sorted(scopy, do_op, do_raw, 1)
+        quantize(do_op, 0, HALF)
+        quantize(do_op, HALF, W)
         group(scopy, dom_op, 0, dom_lo, 0, HALF)
         quantize(dom_op, 0, HALF)
-        product(0, dom_op, 0, pw_op)
-        product(1, dom_op, P, pw_op)
-        gather(v_pairs, v_planes[3], 3)
-        group_pairs(vcopy, v_op, v_pairs, 0, HALF)
-        group_pairs(scopy, v_op, v_pairs, HALF, W)
-        scatter_store(0)
-        scatter_store(1)
-        quantize(v_op, 0, W)
-
-        group_sorted(scopy, do_op, do_raw, 0)
-        group_sorted(scopy, do_op, do_raw, 1)
-        group(vcopy, dom_op, 2 * P, dom_hi, 0, P)
-        group(scopy, dom_op, 3 * P, dom_hi, P, P)
-        quantize(do_op, 0, HALF)
-        quantize(dom_op, 2 * P, 3 * P)
-        score_gradient(1)
-        quantize(do_op, HALF, W)
-        score_gradient(0)
-        quantize(dom_op, 3 * P, W)
-        group(scopy, qm_lo_op, 0, qm_raw, 0, P)
-        score_gradient(3)
-        product(2, dom_op, 2 * P, pw_op)
-        score_gradient(2)
-        group(scopy, qm_lo_op, P, qm_raw, P, P)
-        product(3, dom_op, 3 * P, pw_op)
-        scatter_store(2)
-        group(vcopy, ds_op, 0, ds_rows, 0, HALF)
+        group(scopy, dom_op, HALF, dom_hi, hi0, HALF)
+        quantize(dom_op, HALF, W)
+        for t in range(PACK):
+            score_gradient(t)
+        ds_part(0, 0, W)
+        ds_part(1, 0, W)
+        ds_part(2, HALF, W)
+        ds_part(3, HALF, W)
         group(scopy, ds_op, HALF, ds_rows, HALF, HALF)
-        quantize(qm_lo_op, 0, P)
-        quantize(ds_op, 0, HALF)
+        ds_part(2, 0, HALF)
+        ds_part(3, 0, HALF)
+        group(vcopy, ds_op, 0, ds_rows, 0, HALF)
+        for n in range(PACK):
+            product(n, dom_op, n * P, pw_op)
+            scatter_store(n)
+        group(scopy, qm_op, 0, qm_raw, 0, P)
+        quantize(qm_op, 0, P)
         quantize(ds_op, HALF, W)
-        scatter_store(3)
-
-        product(4, qm_lo_op, 0, ds_op)
-        quantize(qm_lo_op, P, HALF)
+        quantize(ds_op, 0, HALF)
+        product(4, qm_op, 0, ds_op)
         scatter_store(4)
-        product(5, qm_lo_op, P, ds_op)
-        group(scopy, qm_hi_op, 0, qm_raw, HALF, HALF)
-        quantize(qm_hi_op, 0, HALF)
+        qm2 = operand("qm2", E4M3, P, QM2)
+        group(scopy, qm2, 0, qm_raw, P, P)
+        quantize(qm2, 0, P)
+        qm3 = operand("qm3", E4M3, HALF, QM3)
+        group(scopy, qm3, 0, qm_raw, HALF, HALF)
+        quantize(qm3, 0, HALF)
+        product(5, qm2, 0, ds_op)
         scatter_store(5)
-        product(6, qm_hi_op, 0, ds_op)
+        product(6, qm3, 0, ds_op)
         scatter_store(6)
-        product(7, qm_hi_op, P, ds_op)
+        product(7, qm3, P, ds_op)
         scatter_store(7)

@@ -22,16 +22,25 @@ HALF = W // 2
 LIST_ROWS = 16
 ALIGN = 64
 WINDOW_OF = (0, 1, 2, 3, 0, 1, 2, 3)
-LOADS = "k offs gate k k k q v v v dom v do qm"
+LOADS = "k offs gate k k k q v v v dom_lo v do dom_hi qm"
 GV = 4
+DOM0 = 256
+DOM1 = 1
+WHOLE = 2
+DS_DT = F32
+PW_DT = F32
+PW_MODE = "B"
+SQV = 0
+EARLY = 4
+DOV = 0
 PW_IN = "v_plane0"
-QM2 = None
+QM2 = "ds_rows"
 QM3 = "ds_rows"
-DENSE_IN = (None, None, "do_raw", "relu_a", None, None, None, None)
-VK = 320
+DENSE_IN = (None, None, None, "relu_a", None, None, None, None)
+VK = 384
 VQ = 0
-VP = 320
-VV = 192
+VP = 256
+VV = 512
 VS = 256
 
 
@@ -61,6 +70,15 @@ def tile_attend_gat_kv_kernel(tc, qT, kT, vT, doT, rw, qm, dom, offs, out_0, out
 
         def gather(rows, plane, j, lo=0, hi=W):
             vcopy(rows[:, j, lo:hi], plane[:].indirect(offsets[:, lo // LIST_ROWS : hi // LIST_ROWS]))
+
+        def gather_pair(pairs, plane, j):
+            vcopy(pairs[:, j // 2, :, j % 2], plane[:].indirect(offsets[:]))
+
+        def group_pairs(copy, op, pairs, lo, hi):
+            copy(
+                out=op[0][:, lo:hi, :].bitcast(F32).rearrange("p (c i) u -> p c u i", i=2),
+                in_=pairs[:, :, lo:hi, :].rearrange("p u w e -> p u (w e)").bitcast(F32).rearrange("p u (c i) -> p c u i", i=2),
+            )
 
         def group(copy, op, lo, rows, first, count):
             run = 2 if rows.dtype == F32 else 4
@@ -123,12 +141,12 @@ def tile_attend_gat_kv_kernel(tc, qT, kT, vT, doT, rw, qm, dom, offs, out_0, out
         q_op, k_op, pw_op, dom_op = operand("q", E4M3), operand("k", E4M3), operand("pw", E4M3), operand("dom", E5M2)
         do_op, v_op, ds_op, qm_op = operand("do", E5M2), operand("v", E4M3), operand("ds", E5M2), operand("qm", E4M3, P)
         windows = [keep.tile([P, TOKENS], F32, name="window%d" % n) for n in range(max(WINDOW_OF) + 1)]
-        k_rows = keep.tile([P, PACK, W], BF16, name="k_rows", align_bytes=ALIGN)
-        v_rows = keep.tile([P, PACK, W], BF16, name="v_rows", align_bytes=ALIGN)
+        k_rows = keep.tile([P, 2, W, 2], BF16, name="k_rows", align_bytes=ALIGN)
+        v_rows = keep.tile([P, 2, W, 2], BF16, name="v_rows", align_bytes=ALIGN)
         relu_a = keep.tile([P, PACK, W], F32, name="relu_a", align_bytes=ALIGN)
         gate2 = keep.tile([P, PACK], F32, name="gate2")
-        ds_rows = keep.tile([P, PACK, W], BF16, name="ds_rows", align_bytes=ALIGN)
-        pw_rows = keep.tile([P, PACK, W], BF16, name="pw_rows", tag=PW_IN or "pw_rows", align_bytes=ALIGN)
+        ds_rows = keep.tile([P, PACK, W], DS_DT, name="ds_rows", align_bytes=ALIGN)
+        pw_rows = keep.tile([P, PACK, W], PW_DT, name="pw_rows", tag=(PW_IN if PW_MODE == "B" else None) or "pw_rows", align_bytes=ALIGN)
         dense, dp_banks = {}, {}
 
         def weights(t):
@@ -136,6 +154,23 @@ def tile_attend_gat_kv_kernel(tc, qT, kT, vT, doT, rw, qm, dom, offs, out_0, out
             matmul(bank[:], q_op, t * P, k_op, 0, W)
             nc.scalar.activation(relu_a[:, t, :], bank[:], ACT.Relu)
             nc.vector.scalar_tensor_tensor(pw_rows[:, t, :], bank[:], gate[:, t : t + 1], relu_a[:, t, :], MULT, MULT)
+
+        def weights_chunk(c):
+            bank = psum.tile([P, PACK, P], F32, name="score%d" % c, tag="first%d" % c)
+            for t in range(PACK):
+                matmul(bank[:, t, :], q_op, t * P, k_op, c * P, (c + 1) * P)
+            nc.scalar.activation(relu_a[:, :, c * P : (c + 1) * P], bank[:], ACT.Relu)
+            square = keep.tile([P, P, PACK], F32, name="square%d" % c, tag=(PW_IN if c == 0 else None) or "square%d" % c, align_bytes=ALIGN)
+            if c < SQV:
+                rows = relu_a[:, :, c * P : (c + 1) * P].rearrange("p t i -> p i t")
+                nc.vector.tensor_tensor(square[:], rows, rows, MULT)
+            else:
+                nc.scalar.activation(
+                    square[:].rearrange("p (c i) t -> p c t i", i=2),
+                    relu_a[:, :, c * P : (c + 1) * P].rearrange("p t (c i) -> p c t i", i=2),
+                    ACT.Square,
+                )
+            nc.vector.tensor_tensor(pw_op[0][:, c * P : (c + 1) * P, :], square[:], gate[:].unsqueeze(1).to_broadcast([P, P, PACK]), MULT)
 
         def score_gradient(t):
             dp_banks[t] = psum.tile([P, W], F32, name="dp%d" % t, tag="first%d" % t)
@@ -159,46 +194,68 @@ def tile_attend_gat_kv_kernel(tc, qT, kT, vT, doT, rw, qm, dom, offs, out_0, out
             nc.vector.memset(window[:], 0.0)
         nc.vector.tensor_scalar(gate2[:], gate[:], 2.0, None, MULT)
         for j in range(PACK):
-            gather(k_rows, k_planes[j], j)
-        group(vcopy, k_op, 0, k_rows, 0, VK)
-        group(scopy, k_op, VK, k_rows, VK, W - VK)
+            gather_pair(k_rows, k_planes[j], j)
+        group_pairs(vcopy, k_op, k_rows, 0, VK)
+        if VK < W:
+            group_pairs(scopy, k_op, k_rows, VK, W)
         quantize(k_op, 0, W)
-        group_sorted(vcopy, q_op, q_raw, 0)
-        group_sorted(scopy, q_op, q_raw, 1)
+        group_sorted(vcopy if VQ == 0 else scopy, q_op, q_raw, 0)
+        group_sorted(vcopy if VQ == 1 else scopy, q_op, q_raw, 1)
         quantize(q_op, 0, HALF)
         quantize(q_op, HALF, W)
         for j in range(GV):
-            gather(v_rows, v_planes[j], j)
-        for t in range(PACK):
-            weights(t)
-        group(vcopy, pw_op, 0, pw_rows, 0, VP)
-        group(scopy, pw_op, VP, pw_rows, VP, W - VP)
+            gather_pair(v_rows, v_planes[j], j)
+        if PW_MODE == "B":
+            for t in range(PACK):
+                weights(t)
+            group(vcopy, pw_op, 0, pw_rows, 0, VP)
+            group(scopy, pw_op, VP, pw_rows, VP, W - VP)
+        else:
+            for c in range(PACK):
+                weights_chunk(c)
         quantize(pw_op, 0, HALF)
         quantize(pw_op, HALF, W)
         for j in range(GV, PACK):
-            gather(v_rows, v_planes[j], j)
-        group(vcopy, v_op, 0, v_rows, 0, VV)
-        group(scopy, v_op, VV, v_rows, VV, W - VV)
+            gather_pair(v_rows, v_planes[j], j)
+        if VV:
+            group_pairs(vcopy, v_op, v_rows, 0, VV)
+        if VV < W:
+            group_pairs(scopy, v_op, v_rows, VV, W)
         quantize(v_op, 0, W)
-        group_sorted(vcopy, do_op, do_raw, 0)
-        group_sorted(scopy, do_op, do_raw, 1)
+        group_sorted(vcopy if DOV == 1 else scopy, do_op, do_raw, 0)
+        group_sorted(vcopy if DOV == 2 else scopy, do_op, do_raw, 1)
         quantize(do_op, 0, HALF)
         quantize(do_op, HALF, W)
-        group(scopy, dom_op, 0, dom_lo, 0, HALF)
-        quantize(dom_op, 0, HALF)
-        group(scopy, dom_op, HALF, dom_hi, hi0, HALF)
-        quantize(dom_op, HALF, W)
+        if DOM0 < HALF:
+            group(scopy, dom_op, 0, dom_lo, 0, DOM0)
+            quantize(dom_op, 0, P)
+            group(scopy, dom_op, DOM0, dom_lo, DOM0, HALF - DOM0)
+            quantize(dom_op, P, HALF)
+        else:
+            group(scopy, dom_op, 0, dom_lo, 0, HALF)
+            quantize(dom_op, 0, HALF)
+        if DOM1:
+            group(scopy, dom_op, HALF, dom_hi, hi0, P)
+            quantize(dom_op, HALF, 3 * P)
+            group(scopy, dom_op, 3 * P, dom_hi, hi0 + P, P)
+            quantize(dom_op, 3 * P, W)
+        else:
+            group(scopy, dom_op, HALF, dom_hi, hi0, HALF)
+            quantize(dom_op, HALF, W)
+        for n in range(EARLY):
+            product(n, dom_op, n * P, pw_op)
+            scatter_store(n)
         for t in range(PACK):
             score_gradient(t)
-        ds_part(0, 0, W)
-        ds_part(1, 0, W)
-        ds_part(2, HALF, W)
-        ds_part(3, HALF, W)
-        group(scopy, ds_op, HALF, ds_rows, HALF, HALF)
-        ds_part(2, 0, HALF)
-        ds_part(3, 0, HALF)
-        group(vcopy, ds_op, 0, ds_rows, 0, HALF)
-        for n in range(PACK):
+        for t in range(WHOLE):
+            ds_part(t, 0, W)
+        for t in range(WHOLE, PACK):
+            ds_part(t, VS, W)
+        group(scopy, ds_op, VS, ds_rows, VS, W - VS)
+        for t in range(WHOLE, PACK):
+            ds_part(t, 0, VS)
+        group(vcopy, ds_op, 0, ds_rows, 0, VS)
+        for n in range(EARLY, PACK):
             product(n, dom_op, n * P, pw_op)
             scatter_store(n)
         group(scopy, qm_op, 0, qm_raw, 0, P)

@@ -14,34 +14,15 @@ U8 = mybir.dt.uint8
 E4M3 = mybir.dt.float8_e4m3fn_x4
 E5M2 = mybir.dt.float8_e5m2_x4
 MULT = mybir.AluOpType.mult
-ACT = mybir.ActivationFunctionType
+RELU = mybir.ActivationFunctionType.Relu
 
 P = 128
 PACK = 4
 HALF = W // 2
 LIST_ROWS = 16
 ALIGN = 64
-WINDOW_OF = (0, 1, 2, 3, 0, 1, 2, 3)
-LOADS = "k offs gate k k k q v v v dom_lo v do dom_hi qm"
-GV = 4
-DOM0 = 256
-DOM1 = 1
-WHOLE = 2
-DS_DT = F32
-PW_DT = F32
-PW_MODE = "B"
-SQV = 0
-EARLY = 4
-DOV = 0
-PW_IN = "v_plane0"
-QM2 = "ds_rows"
-QM3 = "ds_rows"
-DENSE_IN = (None, None, None, "relu_a", None, None, None, None)
-VK = 384
-VQ = 0
-VP = 256
-VV = 512
-VS = 256
+WINDOWS = 4
+K_ON_VECTOR = 3 * P
 
 
 def tile_attend_gat_kv_kernel(tc, qT, kT, vT, doT, rw, qm, dom, offs, out_0, out_1):
@@ -57,10 +38,11 @@ def tile_attend_gat_kv_kernel(tc, qT, kT, vT, doT, rw, qm, dom, offs, out_0, out
             nc.sync.dma_start(out=raw[:], in_=src.rearrange("(p j) w -> p j w", j=PACK)[:, :, lo:hi])
             return raw
 
-        def load_plane(name, pool_hbm, j):
-            plane = keep.tile([P, TOKENS], F32, name=name, align_bytes=ALIGN)
-            nc.sync.dma_start(out=plane[:], in_=pool_hbm.rearrange("(p j) w -> p j w", j=PACK)[:, j, :])
-            return plane
+        def load_planes(name, pool_hbm, first, count):
+            planes = keep.tile([P, count, TOKENS], F32, name=name, align_bytes=ALIGN)
+            rows = pool_hbm.rearrange("(p j) w -> p j w", j=PACK)[:, first : first + count, :]
+            nc.sync.dma_start(out=planes[:], in_=rows)
+            return [planes[:, i, :] for i in range(count)]
 
         def operand(name, fmt, width=W, tag=None):
             grouped = keep.tile([P, width, PACK], BF16, name=name + "_grouped", tag=tag or name, align_bytes=ALIGN)
@@ -68,16 +50,14 @@ def tile_attend_gat_kv_kernel(tc, qT, kT, vT, doT, rw, qm, dom, offs, out_0, out
             scales = keep.tile([P, width], U8, name=name + "_scales", align_bytes=ALIGN)
             return grouped, codes, scales, fmt
 
-        def gather(rows, plane, j, lo=0, hi=W):
-            vcopy(rows[:, j, lo:hi], plane[:].indirect(offsets[:, lo // LIST_ROWS : hi // LIST_ROWS]))
-
-        def gather_pair(pairs, plane, j):
-            vcopy(pairs[:, j // 2, :, j % 2], plane[:].indirect(offsets[:]))
+        def gather(pairs, plane, j):
+            vcopy(pairs[:, j // 2, :, j % 2], plane.indirect(offsets[:]))
 
         def group_pairs(copy, op, pairs, lo, hi):
+            words = pairs[:, :, lo:hi, :].rearrange("p u w e -> p u (w e)").bitcast(F32)
             copy(
                 out=op[0][:, lo:hi, :].bitcast(F32).rearrange("p (c i) u -> p c u i", i=2),
-                in_=pairs[:, :, lo:hi, :].rearrange("p u w e -> p u (w e)").bitcast(F32).rearrange("p u (c i) -> p c u i", i=2),
+                in_=words.rearrange("p u (c i) -> p c u i", i=2),
             )
 
         def group(copy, op, lo, rows, first, count):
@@ -101,178 +81,114 @@ def tile_attend_gat_kv_kernel(tc, qT, kT, vT, doT, rw, qm, dom, offs, out_0, out
                 in_=grouped[:, lo:hi, :].rearrange("p w j -> p (w j)"),
             )
 
-        def matmul(out, lhs, m0, rhs, lo, hi):
+        def matmul(bank, lhs, m0, rhs):
             nc.tensor.matmul_mx(
-                out=out,
+                out=bank[:],
                 lhsT=lhs[1][:, m0 : m0 + P].bitcast(lhs[3]),
                 lhsT_scale=lhs[2][:, m0 : m0 + P],
-                rhs=rhs[1][:, lo:hi].bitcast(rhs[3]),
-                rhs_scale=rhs[2][:, lo:hi],
+                rhs=rhs[1][:].bitcast(rhs[3]),
+                rhs_scale=rhs[2][:],
                 start=True,
                 stop=True,
             )
 
         offsets = keep.tile([P, W // LIST_ROWS], U16, name="offsets")
         gate = keep.tile([P, PACK], F32, name="gate")
-        raw, k_planes, v_planes = {}, [], []
-        for name in LOADS.split():
-            if name == "offs":
-                nc.sync.dma_start(offsets[:], offs)
-            elif name == "gate":
-                nc.scalar.dma_start(out=gate[:], in_=rw[0].rearrange("(p t) o -> p (t o)", t=PACK))
-            elif name == "k":
-                k_planes.append(load_plane("k_plane%d" % len(k_planes), kT, len(k_planes)))
-            elif name == "v":
-                v_planes.append(load_plane("v_plane%d" % len(v_planes), vT, len(v_planes)))
-            elif name == "q":
-                q_raw = load_rows("q_raw", qT[0], 0, W)
-            elif name == "do":
-                do_raw = load_rows("do_raw", doT[0], 0, W)
-            elif name == "qm":
-                qm_raw = load_rows("qm_raw", qm[0], 0, W)
-            elif name == "dom":
-                dom_raw = load_rows("dom_raw", dom[0], 0, W)
-                dom_lo, dom_hi, hi0 = dom_raw, dom_raw, HALF
-            elif name == "dom_lo":
-                dom_lo = load_rows("dom_lo", dom[0], 0, HALF)
-            elif name == "dom_hi":
-                dom_hi, hi0 = load_rows("dom_hi", dom[0], HALF, W), 0
+        k_planes = load_planes("k_first", kT, 0, PACK - 1)
+        nc.sync.dma_start(offsets[:], offs)
+        nc.scalar.dma_start(out=gate[:], in_=rw[0].rearrange("(p t) o -> p (t o)", t=PACK))
+        k_planes.extend(load_planes("k_last", kT, PACK - 1, 1))
+        q_raw = load_rows("q_raw", qT[0], 0, W)
+        v_planes = [load_planes("v_plane%d" % j, vT, j, 1)[0] for j in range(PACK - 1)]
+        dom_parts = [(0, HALF, load_rows("dom_tiles01", dom[0], 0, HALF))]
+        v_planes.extend(load_planes("v_plane3", vT, PACK - 1, 1))
+        do_raw = load_rows("do_raw", doT[0], 0, W)
+        dom_parts.append((HALF, P, load_rows("dom_tile2", dom[0], HALF, 3 * P)))
+        qm_raw = load_rows("qm_raw", qm[0], 0, W)
+        dom_parts.append((3 * P, P, load_rows("dom_tile3", dom[0], 3 * P, W)))
 
         q_op, k_op, pw_op, dom_op = operand("q", E4M3), operand("k", E4M3), operand("pw", E4M3), operand("dom", E5M2)
-        do_op, v_op, ds_op, qm_op = operand("do", E5M2), operand("v", E4M3), operand("ds", E5M2), operand("qm", E4M3, P)
-        windows = [keep.tile([P, TOKENS], F32, name="window%d" % n) for n in range(max(WINDOW_OF) + 1)]
-        k_rows = keep.tile([P, 2, W, 2], BF16, name="k_rows", align_bytes=ALIGN)
-        v_rows = keep.tile([P, 2, W, 2], BF16, name="v_rows", align_bytes=ALIGN)
+        do_op, v_op, ds_op = operand("do", E5M2), operand("v", E4M3), operand("ds", E5M2)
+        qm_first = operand("qm_first", E4M3, P)
+        windows = [keep.tile([P, TOKENS], F32, name="window%d" % n) for n in range(WINDOWS)]
+        k_pairs = keep.tile([P, 2, W, 2], BF16, name="k_pairs", align_bytes=ALIGN)
+        v_pairs = keep.tile([P, 2, W, 2], BF16, name="v_pairs", align_bytes=ALIGN)
         relu_a = keep.tile([P, PACK, W], F32, name="relu_a", align_bytes=ALIGN)
         gate2 = keep.tile([P, PACK], F32, name="gate2")
-        ds_rows = keep.tile([P, PACK, W], DS_DT, name="ds_rows", align_bytes=ALIGN)
-        pw_rows = keep.tile([P, PACK, W], PW_DT, name="pw_rows", tag=(PW_IN if PW_MODE == "B" else None) or "pw_rows", align_bytes=ALIGN)
-        dense, dp_banks = {}, {}
+        ds_rows = keep.tile([P, PACK, W], BF16, name="ds_rows", tag="do", align_bytes=ALIGN)
+        pw_rows = keep.tile([P, PACK, W], BF16, name="pw_rows", tag="v_plane0", align_bytes=ALIGN)
 
-        def weights(t):
-            bank = psum.tile([P, W], F32, name="score%d" % t, tag="first%d" % t)
-            matmul(bank[:], q_op, t * P, k_op, 0, W)
-            nc.scalar.activation(relu_a[:, t, :], bank[:], ACT.Relu)
-            nc.vector.scalar_tensor_tensor(pw_rows[:, t, :], bank[:], gate[:, t : t + 1], relu_a[:, t, :], MULT, MULT)
-
-        def weights_chunk(c):
-            bank = psum.tile([P, PACK, P], F32, name="score%d" % c, tag="first%d" % c)
-            for t in range(PACK):
-                matmul(bank[:, t, :], q_op, t * P, k_op, c * P, (c + 1) * P)
-            nc.scalar.activation(relu_a[:, :, c * P : (c + 1) * P], bank[:], ACT.Relu)
-            square = keep.tile([P, P, PACK], F32, name="square%d" % c, tag=(PW_IN if c == 0 else None) or "square%d" % c, align_bytes=ALIGN)
-            if c < SQV:
-                rows = relu_a[:, :, c * P : (c + 1) * P].rearrange("p t i -> p i t")
-                nc.vector.tensor_tensor(square[:], rows, rows, MULT)
-            else:
-                nc.scalar.activation(
-                    square[:].rearrange("p (c i) t -> p c t i", i=2),
-                    relu_a[:, :, c * P : (c + 1) * P].rearrange("p t (c i) -> p c t i", i=2),
-                    ACT.Square,
-                )
-            nc.vector.tensor_tensor(pw_op[0][:, c * P : (c + 1) * P, :], square[:], gate[:].unsqueeze(1).to_broadcast([P, P, PACK]), MULT)
-
-        def score_gradient(t):
-            dp_banks[t] = psum.tile([P, W], F32, name="dp%d" % t, tag="first%d" % t)
-            matmul(dp_banks[t][:], do_op, t * P, v_op, 0, W)
-
-        def ds_part(t, lo, hi):
-            nc.vector.scalar_tensor_tensor(ds_rows[:, t, lo:hi], dp_banks[t][:, lo:hi], gate2[:, t : t + 1], relu_a[:, t, lo:hi], MULT, MULT)
-
-        def product(n, lhs, m0, rhs):
+        def output_tile(n, lhs, m0, rhs, tag=None):
             bank = psum.tile([P, W], F32, name="product%d" % n, tag="second%d" % (n % PACK))
-            matmul(bank[:], lhs, m0, rhs, 0, W)
-            dense[n] = keep.tile([P, W], F32, name="dense%d" % n, tag=DENSE_IN[n] or "dense%d" % (n % PACK), align_bytes=ALIGN)
-            scopy(out=dense[n][:], in_=bank[:])
-
-        def scatter_store(n):
-            window, out, row = windows[WINDOW_OF[n]], out_1 if n < PACK else out_0, n % PACK * P
-            vcopy(window[:].indirect(offsets[:]), dense[n][:])
+            matmul(bank, lhs, m0, rhs)
+            dense = keep.tile([P, W], F32, name="dense%d" % n, tag=tag or "dense%d" % (n % PACK), align_bytes=ALIGN)
+            scopy(out=dense[:], in_=bank[:])
+            window, out, row = windows[n % WINDOWS], out_1 if n < PACK else out_0, n % PACK * P
+            vcopy(window[:].indirect(offsets[:]), dense[:])
             nc.sync.dma_start(out=out[row : row + P, :], in_=window[:])
 
         for window in windows:
             nc.vector.memset(window[:], 0.0)
         nc.vector.tensor_scalar(gate2[:], gate[:], 2.0, None, MULT)
+
         for j in range(PACK):
-            gather_pair(k_rows, k_planes[j], j)
-        group_pairs(vcopy, k_op, k_rows, 0, VK)
-        if VK < W:
-            group_pairs(scopy, k_op, k_rows, VK, W)
+            gather(k_pairs, k_planes[j], j)
+        group_pairs(vcopy, k_op, k_pairs, 0, K_ON_VECTOR)
+        group_pairs(scopy, k_op, k_pairs, K_ON_VECTOR, W)
         quantize(k_op, 0, W)
-        group_sorted(vcopy if VQ == 0 else scopy, q_op, q_raw, 0)
-        group_sorted(vcopy if VQ == 1 else scopy, q_op, q_raw, 1)
+        group_sorted(vcopy, q_op, q_raw, 0)
+        group_sorted(scopy, q_op, q_raw, 1)
         quantize(q_op, 0, HALF)
         quantize(q_op, HALF, W)
-        for j in range(GV):
-            gather_pair(v_rows, v_planes[j], j)
-        if PW_MODE == "B":
-            for t in range(PACK):
-                weights(t)
-            group(vcopy, pw_op, 0, pw_rows, 0, VP)
-            group(scopy, pw_op, VP, pw_rows, VP, W - VP)
-        else:
-            for c in range(PACK):
-                weights_chunk(c)
+
+        for j in range(PACK):
+            gather(v_pairs, v_planes[j], j)
+
+        for t in range(PACK):
+            bank = psum.tile([P, W], F32, name="score%d" % t, tag="first%d" % t)
+            matmul(bank, q_op, t * P, k_op)
+            nc.scalar.activation(relu_a[:, t, :], bank[:], RELU)
+            nc.vector.scalar_tensor_tensor(pw_rows[:, t, :], bank[:], gate[:, t : t + 1], relu_a[:, t, :], MULT, MULT)
+        group(vcopy, pw_op, 0, pw_rows, 0, HALF)
+        group(scopy, pw_op, HALF, pw_rows, HALF, HALF)
         quantize(pw_op, 0, HALF)
         quantize(pw_op, HALF, W)
-        for j in range(GV, PACK):
-            gather_pair(v_rows, v_planes[j], j)
-        if VV:
-            group_pairs(vcopy, v_op, v_rows, 0, VV)
-        if VV < W:
-            group_pairs(scopy, v_op, v_rows, VV, W)
+
+        group_pairs(vcopy, v_op, v_pairs, 0, HALF)
+        group_pairs(scopy, v_op, v_pairs, HALF, W)
         quantize(v_op, 0, W)
-        group_sorted(vcopy if DOV == 1 else scopy, do_op, do_raw, 0)
-        group_sorted(vcopy if DOV == 2 else scopy, do_op, do_raw, 1)
-        quantize(do_op, 0, HALF)
-        quantize(do_op, HALF, W)
-        if DOM0 < HALF:
-            group(scopy, dom_op, 0, dom_lo, 0, DOM0)
-            quantize(dom_op, 0, P)
-            group(scopy, dom_op, DOM0, dom_lo, DOM0, HALF - DOM0)
-            quantize(dom_op, P, HALF)
-        else:
-            group(scopy, dom_op, 0, dom_lo, 0, HALF)
-            quantize(dom_op, 0, HALF)
-        if DOM1:
-            group(scopy, dom_op, HALF, dom_hi, hi0, P)
-            quantize(dom_op, HALF, 3 * P)
-            group(scopy, dom_op, 3 * P, dom_hi, hi0 + P, P)
-            quantize(dom_op, 3 * P, W)
-        else:
-            group(scopy, dom_op, HALF, dom_hi, hi0, HALF)
-            quantize(dom_op, HALF, W)
-        for n in range(EARLY):
-            product(n, dom_op, n * P, pw_op)
-            scatter_store(n)
+        for half in range(2):
+            group_sorted(scopy, do_op, do_raw, half)
+        for half in range(2):
+            quantize(do_op, half * HALF, (half + 1) * HALF)
+        for lo, count, part in dom_parts:
+            group(scopy, dom_op, lo, part, 0, count)
+            quantize(dom_op, lo, lo + count)
+
+        dp_banks = [psum.tile([P, W], F32, name="dp%d" % t, tag="first%d" % t) for t in range(PACK)]
         for t in range(PACK):
-            score_gradient(t)
-        for t in range(WHOLE):
-            ds_part(t, 0, W)
-        for t in range(WHOLE, PACK):
-            ds_part(t, VS, W)
-        group(scopy, ds_op, VS, ds_rows, VS, W - VS)
-        for t in range(WHOLE, PACK):
-            ds_part(t, 0, VS)
-        group(vcopy, ds_op, 0, ds_rows, 0, VS)
-        for n in range(EARLY, PACK):
-            product(n, dom_op, n * P, pw_op)
-            scatter_store(n)
-        group(scopy, qm_op, 0, qm_raw, 0, P)
-        quantize(qm_op, 0, P)
+            matmul(dp_banks[t], do_op, t * P, v_op)
+        for t in range(PACK):
+            nc.vector.scalar_tensor_tensor(
+                ds_rows[:, t, :], dp_banks[t][:], gate2[:, t : t + 1], relu_a[:, t, :], MULT, MULT
+            )
+        group(scopy, ds_op, HALF, ds_rows, HALF, HALF)
+        group(vcopy, ds_op, 0, ds_rows, 0, HALF)
+
+        for n in range(PACK):
+            output_tile(n, dom_op, n * P, pw_op, "relu_a" if n == PACK - 1 else None)
+
+        group(scopy, qm_first, 0, qm_raw, 0, P)
+        quantize(qm_first, 0, P)
         quantize(ds_op, HALF, W)
         quantize(ds_op, 0, HALF)
-        product(4, qm_op, 0, ds_op)
-        scatter_store(4)
-        qm2 = operand("qm2", E4M3, P, QM2)
-        group(scopy, qm2, 0, qm_raw, P, P)
-        quantize(qm2, 0, P)
-        qm3 = operand("qm3", E4M3, HALF, QM3)
-        group(scopy, qm3, 0, qm_raw, HALF, HALF)
-        quantize(qm3, 0, HALF)
-        product(5, qm2, 0, ds_op)
-        scatter_store(5)
-        product(6, qm3, 0, ds_op)
-        scatter_store(6)
-        product(7, qm3, P, ds_op)
-        scatter_store(7)
+        output_tile(4, qm_first, 0, ds_op)
+        qm_second = operand("qm_second", E4M3, P, "do")
+        group(scopy, qm_second, 0, qm_raw, P, P)
+        quantize(qm_second, 0, P)
+        qm_rest = operand("qm_rest", E4M3, HALF, "do")
+        group(scopy, qm_rest, 0, qm_raw, HALF, HALF)
+        quantize(qm_rest, 0, HALF)
+        output_tile(5, qm_second, 0, ds_op)
+        output_tile(6, qm_rest, 0, ds_op)
+        output_tile(7, qm_rest, P, ds_op)

@@ -22,7 +22,7 @@ HALF = W // 2
 LIST_ROWS = 16
 ALIGN = 64
 WINDOWS = 4
-K_ON_VECTOR = 3 * P
+PAIRS_ON_VECTOR = 3 * P
 
 
 def tile_attend_gat_kv_kernel(tc, qT, kT, vT, doT, rw, qm, dom, offs, out_0, out_1):
@@ -94,10 +94,11 @@ def tile_attend_gat_kv_kernel(tc, qT, kT, vT, doT, rw, qm, dom, offs, out_0, out
 
         offsets = keep.tile([P, W // LIST_ROWS], U16, name="offsets")
         gate = keep.tile([P, PACK], F32, name="gate")
-        k_planes = load_planes("k_first", kT, 0, PACK - 1)
+        k_planes = load_planes("k_planes01", kT, 0, 2)
         nc.sync.dma_start(offsets[:], offs)
         nc.scalar.dma_start(out=gate[:], in_=rw[0].rearrange("(p t) o -> p (t o)", t=PACK))
-        k_planes.extend(load_planes("k_last", kT, PACK - 1, 1))
+        for j in range(2, PACK):
+            k_planes.extend(load_planes("k_plane%d" % j, kT, j, 1))
         q_raw = load_rows("q_raw", qT[0], 0, W)
         v_planes = [load_planes("v_plane%d" % j, vT, j, 1)[0] for j in range(PACK - 1)]
         dom_parts = [(0, HALF, load_rows("dom_tiles01", dom[0], 0, HALF))]
@@ -133,8 +134,8 @@ def tile_attend_gat_kv_kernel(tc, qT, kT, vT, doT, rw, qm, dom, offs, out_0, out
 
         for j in range(PACK):
             gather(k_pairs, k_planes[j], j)
-        group_pairs(vcopy, k_op, k_pairs, 0, K_ON_VECTOR)
-        group_pairs(scopy, k_op, k_pairs, K_ON_VECTOR, W)
+        group_pairs(vcopy, k_op, k_pairs, 0, PAIRS_ON_VECTOR)
+        group_pairs(scopy, k_op, k_pairs, PAIRS_ON_VECTOR, W)
         quantize(k_op, 0, W)
         group_sorted(vcopy, q_op, q_raw, 0)
         group_sorted(scopy, q_op, q_raw, 1)
@@ -154,8 +155,8 @@ def tile_attend_gat_kv_kernel(tc, qT, kT, vT, doT, rw, qm, dom, offs, out_0, out
         quantize(pw_op, 0, HALF)
         quantize(pw_op, HALF, W)
 
-        group_pairs(vcopy, v_op, v_pairs, 0, HALF)
-        group_pairs(scopy, v_op, v_pairs, HALF, W)
+        group_pairs(vcopy, v_op, v_pairs, 0, PAIRS_ON_VECTOR)
+        group_pairs(scopy, v_op, v_pairs, PAIRS_ON_VECTOR, W)
         quantize(v_op, 0, W)
         for half in range(2):
             group_sorted(scopy, do_op, do_raw, half)

@@ -15,6 +15,7 @@ E4M3 = mybir.dt.float8_e4m3fn_x4
 E5M2 = mybir.dt.float8_e5m2_x4
 MULT = mybir.AluOpType.mult
 RELU = mybir.ActivationFunctionType.Relu
+COPY = mybir.ActivationFunctionType.Copy
 
 P = 128
 PACK = 4
@@ -50,13 +51,13 @@ def tile_attend_gat_kv_kernel(tc, qT, kT, vT, doT, rw, qm, dom, offs, out_0, out
             scales = keep.tile([P, width], U8, name=name + "_scales", align_bytes=ALIGN)
             return grouped, codes, scales, fmt
 
-        def gather(pairs, plane, j):
-            vcopy(pairs[:, j // 2, :, j % 2], plane.indirect(offsets[:]))
+        def gather(pairs, plane, j, lo, hi):
+            vcopy(pairs[:, j // 2, :, j % 2], plane.indirect(offsets[:, lo // LIST_ROWS : hi // LIST_ROWS]))
 
-        def group_pairs(copy, op, pairs, lo, hi):
-            words = pairs[:, :, lo:hi, :].rearrange("p u w e -> p u (w e)").bitcast(F32)
+        def group_pairs(copy, op, lo, pairs, first, count):
+            words = pairs[:, :, first : first + count, :].rearrange("p u w e -> p u (w e)").bitcast(F32)
             copy(
-                out=op[0][:, lo:hi, :].bitcast(F32).rearrange("p (c i) u -> p c u i", i=2),
+                out=op[0][:, lo : lo + count, :].bitcast(F32).rearrange("p (c i) u -> p c u i", i=2),
                 in_=words.rearrange("p u (c i) -> p c u i", i=2),
             )
 
@@ -67,10 +68,10 @@ def tile_attend_gat_kv_kernel(tc, qT, kT, vT, doT, rw, qm, dom, offs, out_0, out
                 in_=rows[:, :, first : first + count].rearrange("p j (c i) -> p c j i", i=run),
             )
 
-        def group_sorted(copy, op, rows, half):
+        def group_sorted(copy, op, rows, first, count):
             copy(
-                out=op[0][:, half * HALF : (half + 1) * HALF, :].rearrange("p (t m) j -> p m j t", t=2),
-                in_=rows[:].rearrange("p j (m t) -> p m j t", t=PACK)[:, :, :, 2 * half : 2 * half + 2],
+                out=op[0][:, first * P : (first + count) * P, :].rearrange("p (t m) j -> p m j t", t=count),
+                in_=rows[:].rearrange("p j (m t) -> p m j t", t=PACK)[:, :, :, first : first + count],
             )
 
         def quantize(op, lo, hi):
@@ -81,13 +82,13 @@ def tile_attend_gat_kv_kernel(tc, qT, kT, vT, doT, rw, qm, dom, offs, out_0, out
                 in_=grouped[:, lo:hi, :].rearrange("p w j -> p (w j)"),
             )
 
-        def matmul(bank, lhs, m0, rhs):
+        def matmul(out, lhs, m0, rhs, lo, hi):
             nc.tensor.matmul_mx(
-                out=bank[:],
+                out=out,
                 lhsT=lhs[1][:, m0 : m0 + P].bitcast(lhs[3]),
                 lhsT_scale=lhs[2][:, m0 : m0 + P],
-                rhs=rhs[1][:].bitcast(rhs[3]),
-                rhs_scale=rhs[2][:],
+                rhs=rhs[1][:, lo:hi].bitcast(rhs[3]),
+                rhs_scale=rhs[2][:, lo:hi],
                 start=True,
                 stop=True,
             )
@@ -100,96 +101,141 @@ def tile_attend_gat_kv_kernel(tc, qT, kT, vT, doT, rw, qm, dom, offs, out_0, out
         for j in range(2, PACK):
             k_planes.extend(load_planes("k_plane%d" % j, kT, j, 1))
         q_raw = load_rows("q_raw", qT[0], 0, W)
-        v_planes = [load_planes("v_plane%d" % j, vT, j, 1)[0] for j in range(PACK - 1)]
-        dom_parts = [(0, HALF, load_rows("dom_tiles01", dom[0], 0, HALF))]
-        v_planes.extend(load_planes("v_plane3", vT, PACK - 1, 1))
+        v_planes = load_planes("v_plane0", vT, 0, 1)
+        dom_raw = load_rows("dom_raw", dom[0], 0, W)
+        for j in range(1, PACK):
+            v_planes.extend(load_planes("v_plane%d" % j, vT, j, 1))
         do_raw = load_rows("do_raw", doT[0], 0, W)
-        dom_parts.append((HALF, P, load_rows("dom_tile2", dom[0], HALF, 3 * P)))
         qm_raw = load_rows("qm_raw", qm[0], 0, W)
-        dom_parts.append((3 * P, P, load_rows("dom_tile3", dom[0], 3 * P, W)))
 
-        q_op, k_op, pw_op, dom_op = operand("q", E4M3), operand("k", E4M3), operand("pw", E4M3), operand("dom", E5M2)
+        q_op, k_op, pw_op = operand("q", E4M3), operand("k", E4M3), operand("pw", E4M3)
         do_op, v_op, ds_op = operand("do", E5M2), operand("v", E4M3), operand("ds", E5M2)
+        dom_ops = [operand("dom%d" % n, E5M2, P) for n in range(PACK)]
         qm_first = operand("qm_first", E4M3, P)
         windows = [keep.tile([P, TOKENS], F32, name="window%d" % n) for n in range(WINDOWS)]
         k_pairs = keep.tile([P, 2, W, 2], BF16, name="k_pairs", align_bytes=ALIGN)
-        v_pairs = keep.tile([P, 2, W, 2], BF16, name="v_pairs", align_bytes=ALIGN)
-        relu_a = keep.tile([P, PACK, W], F32, name="relu_a", align_bytes=ALIGN)
+        relu_a = [keep.tile([P, 2, HALF], F32, name="relu_a%d" % i, align_bytes=ALIGN) for i in range(PACK)]
         gate2 = keep.tile([P, PACK], F32, name="gate2")
-        ds_rows = keep.tile([P, PACK, W], BF16, name="ds_rows", tag="do", align_bytes=ALIGN)
-        pw_rows = keep.tile([P, PACK, W], BF16, name="pw_rows", tag="v_plane0", align_bytes=ALIGN)
+        ds_rows = [keep.tile([P, PACK, HALF], BF16, name="ds_rows%d" % h, align_bytes=ALIGN) for h in range(2)]
+        pw_rows = [keep.tile([P, PACK, HALF], BF16, name="pw_rows%d" % h, align_bytes=ALIGN) for h in range(2)]
 
-        def output_tile(n, lhs, m0, rhs, tag=None):
-            bank = psum.tile([P, W], F32, name="product%d" % n, tag="second%d" % (n % PACK))
-            matmul(bank, lhs, m0, rhs)
-            dense = keep.tile([P, W], F32, name="dense%d" % n, tag=tag or "dense%d" % (n % PACK), align_bytes=ALIGN)
-            scopy(out=dense[:], in_=bank[:])
-            window, out, row = windows[n % WINDOWS], out_1 if n < PACK else out_0, n % PACK * P
-            vcopy(window[:].indirect(offsets[:]), dense[:])
-            nc.sync.dma_start(out=out[row : row + P, :], in_=window[:])
+        def scatter(n, dense, lo, hi, on_scalar):
+            part = offsets[:, lo // LIST_ROWS : hi // LIST_ROWS]
+            if on_scalar:
+                nc.scalar.activation(windows[n % WINDOWS][:].indirect(part), dense[:], COPY)
+            else:
+                vcopy(windows[n % WINDOWS][:].indirect(part), dense[:])
+
+        def product(n, lhs, rhs, lo, hi, bank_tag, dense):
+            bank = psum.tile([P, hi - lo], F32, name="product%d_%d" % (n, lo), tag=bank_tag)
+            matmul(bank[:], lhs[0], lhs[1], rhs, lo, hi)
+            scopy(out=dense, in_=bank[:])
+
+        def dense_tile(name, width, tag):
+            return keep.tile([P, width], F32, name=name, tag=tag, align_bytes=ALIGN)
+
+        def store(n):
+            out, row = out_1 if n < PACK else out_0, n % PACK * P
+            nc.sync.dma_start(out=out[row : row + P, :], in_=windows[n % WINDOWS][:])
+
+        def output_tile(n, lhs, rhs, on_scalar, bank_tag, dense):
+            product(n, lhs, rhs, 0, W, bank_tag, dense)
+            if on_scalar:
+                for lo in range(0, W, HALF):
+                    scatter(n, dense[:, lo : lo + HALF], lo, lo + HALF, True)
+            else:
+                scatter(n, dense, 0, W, False)
+            store(n)
 
         for window in windows:
             nc.vector.memset(window[:], 0.0)
         nc.vector.tensor_scalar(gate2[:], gate[:], 2.0, None, MULT)
 
         for j in range(PACK):
-            gather(k_pairs, k_planes[j], j)
-        group_pairs(vcopy, k_op, k_pairs, 0, PAIRS_ON_VECTOR)
-        group_pairs(scopy, k_op, k_pairs, PAIRS_ON_VECTOR, W)
+            gather(k_pairs, k_planes[j], j, 0, W)
+        group_pairs(vcopy, k_op, 0, k_pairs, 0, PAIRS_ON_VECTOR)
+        group_pairs(scopy, k_op, PAIRS_ON_VECTOR, k_pairs, PAIRS_ON_VECTOR, W - PAIRS_ON_VECTOR)
         quantize(k_op, 0, W)
-        group_sorted(vcopy, q_op, q_raw, 0)
-        group_sorted(scopy, q_op, q_raw, 1)
+        group_sorted(vcopy, q_op, q_raw, 0, 2)
+        group_sorted(scopy, q_op, q_raw, 2, 2)
         quantize(q_op, 0, HALF)
         quantize(q_op, HALF, W)
 
-        for j in range(PACK):
-            gather(v_pairs, v_planes[j], j)
-
-        for t in range(PACK):
-            bank = psum.tile([P, W], F32, name="score%d" % t, tag="first%d" % t)
-            matmul(bank, q_op, t * P, k_op)
-            nc.scalar.activation(relu_a[:, t, :], bank[:], RELU)
-            nc.vector.scalar_tensor_tensor(pw_rows[:, t, :], bank[:], gate[:, t : t + 1], relu_a[:, t, :], MULT, MULT)
-        group(vcopy, pw_op, 0, pw_rows, 0, HALF)
-        group(scopy, pw_op, HALF, pw_rows, HALF, HALF)
+        a_banks = [psum.tile([P, 2, HALF], F32, name="score%d" % i, tag="first%d" % i) for i in range(PACK)]
+        for h in range(2):
+            for t in range(PACK):
+                matmul(a_banks[2 * h + t // 2][:, t % 2, :], q_op, t * P, k_op, h * HALF, (h + 1) * HALF)
+        for i in range(PACK):
+            nc.scalar.activation(relu_a[i][:], a_banks[i][:], RELU)
+        for h in range(2):
+            for t in range(PACK):
+                i = 2 * h + t // 2
+                nc.vector.scalar_tensor_tensor(
+                    pw_rows[h][:, t, :], a_banks[i][:, t % 2, :], gate[:, t : t + 1], relu_a[i][:, t % 2, :], MULT, MULT
+                )
+        group(scopy, pw_op, 0, pw_rows[0], 0, HALF)
+        group(vcopy, pw_op, HALF, pw_rows[1], 0, HALF)
         quantize(pw_op, 0, HALF)
         quantize(pw_op, HALF, W)
 
-        group_pairs(vcopy, v_op, v_pairs, 0, PAIRS_ON_VECTOR)
-        group_pairs(scopy, v_op, v_pairs, PAIRS_ON_VECTOR, W)
-        quantize(v_op, 0, W)
-        for half in range(2):
-            group_sorted(scopy, do_op, do_raw, half)
-        for half in range(2):
-            quantize(do_op, half * HALF, (half + 1) * HALF)
-        for lo, count, part in dom_parts:
-            group(scopy, dom_op, lo, part, 0, count)
-            quantize(dom_op, lo, lo + count)
+        for n in range(2):
+            group(scopy, dom_ops[n], 0, dom_raw, n * P, P)
+            quantize(dom_ops[n], 0, P)
+        nc.gpsimd.tensor_copy(out=dom_ops[2][0][:], in_=dom_raw[:, :, HALF : 3 * P].rearrange("p j c -> p c j"))
+        quantize(dom_ops[2], 0, P)
+        group(scopy, dom_ops[3], 0, dom_raw, 3 * P, P)
+        quantize(dom_ops[3], 0, P)
+        v_pairs = [keep.tile([P, 2, HALF, 2], BF16, name="v_pairs%d" % h, align_bytes=ALIGN) for h in range(2)]
 
-        dp_banks = [psum.tile([P, W], F32, name="dp%d" % t, tag="first%d" % t) for t in range(PACK)]
-        for t in range(PACK):
-            matmul(dp_banks[t], do_op, t * P, v_op)
-        for t in range(PACK):
-            nc.vector.scalar_tensor_tensor(
-                ds_rows[:, t, :], dp_banks[t][:], gate2[:, t : t + 1], relu_a[:, t, :], MULT, MULT
-            )
-        group(scopy, ds_op, HALF, ds_rows, HALF, HALF)
-        group(vcopy, ds_op, 0, ds_rows, 0, HALF)
+        for j in range(PACK - 1):
+            for h in range(2):
+                gather(v_pairs[h], v_planes[j], j, h * HALF, (h + 1) * HALF)
+        for h in range(2):
+            gather(v_pairs[h], v_planes[PACK - 1], PACK - 1, h * HALF, (h + 1) * HALF)
+        for h in range(2):
+            group_pairs(vcopy, v_op, h * HALF, v_pairs[h], 0, HALF)
+        for h in range(2):
+            quantize(v_op, h * HALF, (h + 1) * HALF)
+        group_sorted(vcopy, do_op, do_raw, 0, 2)
+        group_sorted(scopy, do_op, do_raw, 2, 2)
+        quantize(do_op, 0, HALF)
+        quantize(do_op, HALF, W)
+
+        dp_banks = [psum.tile([P, 2, HALF], F32, name="dp%d" % i, tag="first%d" % i) for i in range(PACK)]
+        for h in range(2):
+            for t in range(PACK):
+                matmul(dp_banks[2 * h + t // 2][:, t % 2, :], do_op, t * P, v_op, h * HALF, (h + 1) * HALF)
+        for h in range(2):
+            for t in range(PACK):
+                nc.vector.scalar_tensor_tensor(
+                    ds_rows[h][:, t, :],
+                    dp_banks[2 * h + t // 2][:, t % 2, :],
+                    gate2[:, t : t + 1],
+                    relu_a[2 * h + t // 2][:, t % 2, :],
+                    MULT,
+                    MULT,
+                )
+        group(scopy, ds_op, 0, ds_rows[0], 0, HALF)
+        group(vcopy, ds_op, HALF, ds_rows[1], 0, HALF)
 
         for n in range(PACK):
-            output_tile(n, dom_op, n * P, pw_op, "relu_a" if n == PACK - 1 else None)
+            output_tile(n, (dom_ops[n], 0), pw_op, True, "second%d" % n, dense_tile("dense%d" % n, W, "do_raw" if n == PACK - 1 else "dense%d" % (n % 2))[:])
 
-        group(scopy, qm_first, 0, qm_raw, 0, P)
+        group(vcopy, qm_first, 0, qm_raw, 0, P)
         quantize(qm_first, 0, P)
-        quantize(ds_op, HALF, W)
         quantize(ds_op, 0, HALF)
-        output_tile(4, qm_first, 0, ds_op)
-        qm_second = operand("qm_second", E4M3, P, "do")
+        quantize(ds_op, HALF, W)
+        for h in range(2):
+            dense = dense_tile("dense4_%d" % h, HALF, "dense%d" % h)[:]
+            product(4, (qm_first, 0), ds_op, h * HALF, (h + 1) * HALF, "second%d" % h, dense)
+            scatter(4, dense, h * HALF, (h + 1) * HALF, False)
+        store(4)
+        qm_second = operand("qm_second", E4M3, P, "ds_rows0")
         group(scopy, qm_second, 0, qm_raw, P, P)
         quantize(qm_second, 0, P)
-        qm_rest = operand("qm_rest", E4M3, HALF, "do")
+        qm_rest = operand("qm_rest", E4M3, HALF, "dense0")
         group(scopy, qm_rest, 0, qm_raw, HALF, HALF)
         quantize(qm_rest, 0, HALF)
-        output_tile(5, qm_second, 0, ds_op)
-        output_tile(6, qm_rest, 0, ds_op)
-        output_tile(7, qm_rest, P, ds_op)
+        output_tile(5, (qm_second, 0), ds_op, False, "second2", dense_tile("dense5", W, "dense2")[:])
+        output_tile(6, (qm_rest, 0), ds_op, False, "second3", dense_tile("dense6", W, "dense3")[:])
+        output_tile(7, (qm_rest, P), ds_op, False, "second0", dense_tile("dense7", W, "dense0")[:])

from contextlib import ExitStack

import concourse.mybir as mybir

TOKENS = 2048
W = 512
FLOPS = 4 * 2 * W * W * W

F32 = mybir.dt.float32
BF16 = mybir.dt.bfloat16
U32 = mybir.dt.uint32
U16 = mybir.dt.uint16
U8 = mybir.dt.uint8
E4M3 = mybir.dt.float8_e4m3fn_x4
E5M2 = mybir.dt.float8_e5m2_x4
MULT = mybir.AluOpType.mult
RELU = mybir.ActivationFunctionType.Relu
COPY = mybir.ActivationFunctionType.Copy

P = 128
PACK = 4
HALF = W // 2
LIST_ROWS = 16
ALIGN = 64
WINDOWS = 4
PAIRS_ON_VECTOR = 3 * P


def tile_attend_gat_kv_kernel(tc, qT, kT, vT, doT, rw, qm, dom, offs, out_0, out_1):
    nc = tc.nc
    vcopy = nc.vector.tensor_copy
    scopy = nc.scalar.copy
    with ExitStack() as ctx:
        keep = ctx.enter_context(tc.tile_pool(name="keep", bufs=1))
        psum = ctx.enter_context(tc.psum_pool(name="psum", bufs=1))

        def load_rows(name, src, lo, hi):
            raw = keep.tile([P, PACK, hi - lo], F32, name=name, align_bytes=ALIGN)
            nc.sync.dma_start(out=raw[:], in_=src.rearrange("(p j) w -> p j w", j=PACK)[:, :, lo:hi])
            return raw

        def load_planes(name, pool_hbm, first, count):
            planes = keep.tile([P, count, TOKENS], F32, name=name, align_bytes=ALIGN)
            rows = pool_hbm.rearrange("(p j) w -> p j w", j=PACK)[:, first : first + count, :]
            nc.sync.dma_start(out=planes[:], in_=rows)
            return [planes[:, i, :] for i in range(count)]

        def operand(name, fmt, width=W, tag=None):
            grouped = keep.tile([P, width, PACK], BF16, name=name + "_grouped", tag=tag or name, align_bytes=ALIGN)
            codes = keep.tile([P, width], U32, name=name + "_codes", align_bytes=ALIGN)
            scales = keep.tile([P, width], U8, name=name + "_scales", align_bytes=ALIGN)
            return grouped, codes, scales, fmt

        def gather(pairs, plane, j, lo, hi):
            vcopy(pairs[:, j // 2, :, j % 2], plane.indirect(offsets[:, lo // LIST_ROWS : hi // LIST_ROWS]))

        def group_pairs(copy, op, lo, pairs, first, count):
            words = pairs[:, :, first : first + count, :].rearrange("p u w e -> p u (w e)").bitcast(F32)
            copy(
                out=op[0][:, lo : lo + count, :].bitcast(F32).rearrange("p (c i) u -> p c u i", i=2),
                in_=words.rearrange("p u (c i) -> p c u i", i=2),
            )

        def group(copy, op, lo, rows, first, count):
            run = 2 if rows.dtype == F32 else 4
            copy(
                out=op[0][:, lo : lo + count, :].rearrange("p (c i) j -> p c j i", i=run),
                in_=rows[:, :, first : first + count].rearrange("p j (c i) -> p c j i", i=run),
            )

        def group_sorted(copy, op, rows, first, count):
            copy(
                out=op[0][:, first * P : (first + count) * P, :].rearrange("p (t m) j -> p m j t", t=count),
                in_=rows[:].rearrange("p j (m t) -> p m j t", t=PACK)[:, :, :, first : first + count],
            )

        def quantize(op, lo, hi):
            grouped, codes, scales, fmt = op
            nc.vector.quantize_mx(
                out=codes[:, lo:hi].bitcast(fmt),
                scales=scales[:, lo:hi],
                in_=grouped[:, lo:hi, :].rearrange("p w j -> p (w j)"),
            )

        def matmul(out, lhs, m0, rhs, lo, hi):
            nc.tensor.matmul_mx(
                out=out,
                lhsT=lhs[1][:, m0 : m0 + P].bitcast(lhs[3]),
                lhsT_scale=lhs[2][:, m0 : m0 + P],
                rhs=rhs[1][:, lo:hi].bitcast(rhs[3]),
                rhs_scale=rhs[2][:, lo:hi],
                start=True,
                stop=True,
            )

        offsets = keep.tile([P, W // LIST_ROWS], U16, name="offsets")
        gate = keep.tile([P, PACK], F32, name="gate")
        k_planes = load_planes("k_planes01", kT, 0, 2)
        nc.sync.dma_start(offsets[:], offs)
        nc.scalar.dma_start(out=gate[:], in_=rw[0].rearrange("(p t) o -> p (t o)", t=PACK))
        for j in range(2, PACK):
            k_planes.extend(load_planes("k_plane%d" % j, kT, j, 1))
        q_raw = load_rows("q_raw", qT[0], 0, W)
        v_planes = load_planes("v_plane0", vT, 0, 1)
        dom_raw = load_rows("dom_raw", dom[0], 0, W)
        for j in range(1, PACK):
            v_planes.extend(load_planes("v_plane%d" % j, vT, j, 1))
        do_raw = load_rows("do_raw", doT[0], 0, W)
        qm_raw = load_rows("qm_raw", qm[0], 0, W)

        q_op, k_op, pw_op = operand("q", E4M3), operand("k", E4M3), operand("pw", E4M3)
        do_op, v_op, ds_op = operand("do", E5M2), operand("v", E4M3), operand("ds", E5M2)
        dom_ops = [operand("dom%d" % n, E5M2, P) for n in range(PACK)]
        qm_first = operand("qm_first", E4M3, P)
        windows = [keep.tile([P, TOKENS], F32, name="window%d" % n) for n in range(WINDOWS)]
        k_pairs = keep.tile([P, 2, W, 2], BF16, name="k_pairs", align_bytes=ALIGN)
        relu_a = [keep.tile([P, 2, HALF], F32, name="relu_a%d" % i, align_bytes=ALIGN) for i in range(PACK)]
        gate2 = keep.tile([P, PACK], F32, name="gate2")
        ds_rows = [keep.tile([P, PACK, HALF], BF16, name="ds_rows%d" % h, align_bytes=ALIGN) for h in range(2)]
        pw_rows = [keep.tile([P, PACK, HALF], BF16, name="pw_rows%d" % h, align_bytes=ALIGN) for h in range(2)]

        def scatter(n, dense, lo, hi, on_scalar):
            part = offsets[:, lo // LIST_ROWS : hi // LIST_ROWS]
            if on_scalar:
                nc.scalar.activation(windows[n % WINDOWS][:].indirect(part), dense[:], COPY)
            else:
                vcopy(windows[n % WINDOWS][:].indirect(part), dense[:])

        def product(n, lhs, rhs, lo, hi, bank_tag, dense):
            bank = psum.tile([P, hi - lo], F32, name="product%d_%d" % (n, lo), tag=bank_tag)
            matmul(bank[:], lhs[0], lhs[1], rhs, lo, hi)
            scopy(out=dense, in_=bank[:])

        def dense_tile(name, width, tag):
            return keep.tile([P, width], F32, name=name, tag=tag, align_bytes=ALIGN)

        def store(n):
            out, row = out_1 if n < PACK else out_0, n % PACK * P
            nc.sync.dma_start(out=out[row : row + P, :], in_=windows[n % WINDOWS][:])

        def output_tile(n, lhs, rhs, on_scalar, bank_tag, dense):
            product(n, lhs, rhs, 0, W, bank_tag, dense)
            if on_scalar:
                for lo in range(0, W, HALF):
                    scatter(n, dense[:, lo : lo + HALF], lo, lo + HALF, True)
            else:
                scatter(n, dense, 0, W, False)
            store(n)

        for window in windows:
            nc.vector.memset(window[:], 0.0)
        nc.vector.tensor_scalar(gate2[:], gate[:], 2.0, None, MULT)

        for j in range(PACK):
            gather(k_pairs, k_planes[j], j, 0, W)
        group_pairs(vcopy, k_op, 0, k_pairs, 0, PAIRS_ON_VECTOR)
        group_pairs(scopy, k_op, PAIRS_ON_VECTOR, k_pairs, PAIRS_ON_VECTOR, W - PAIRS_ON_VECTOR)
        quantize(k_op, 0, W)
        group_sorted(vcopy, q_op, q_raw, 0, 2)
        group_sorted(scopy, q_op, q_raw, 2, 2)
        quantize(q_op, 0, HALF)
        quantize(q_op, HALF, W)

        a_banks = [psum.tile([P, 2, HALF], F32, name="score%d" % i, tag="first%d" % i) for i in range(PACK)]
        for h in range(2):
            for t in range(PACK):
                matmul(a_banks[2 * h + t // 2][:, t % 2, :], q_op, t * P, k_op, h * HALF, (h + 1) * HALF)
        for i in range(PACK):
            nc.scalar.activation(relu_a[i][:], a_banks[i][:], RELU)
        for h in range(2):
            for t in range(PACK):
                i = 2 * h + t // 2
                nc.vector.scalar_tensor_tensor(
                    pw_rows[h][:, t, :], a_banks[i][:, t % 2, :], gate[:, t : t + 1], relu_a[i][:, t % 2, :], MULT, MULT
                )
        group(scopy, pw_op, 0, pw_rows[0], 0, HALF)
        group(vcopy, pw_op, HALF, pw_rows[1], 0, HALF)
        quantize(pw_op, 0, HALF)
        quantize(pw_op, HALF, W)

        for n in range(2):
            group(scopy, dom_ops[n], 0, dom_raw, n * P, P)
            quantize(dom_ops[n], 0, P)
        nc.gpsimd.tensor_copy(out=dom_ops[2][0][:], in_=dom_raw[:, :, HALF : 3 * P].rearrange("p j c -> p c j"))
        quantize(dom_ops[2], 0, P)
        group(scopy, dom_ops[3], 0, dom_raw, 3 * P, P)
        quantize(dom_ops[3], 0, P)
        v_pairs = [keep.tile([P, 2, HALF, 2], BF16, name="v_pairs%d" % h, align_bytes=ALIGN) for h in range(2)]

        for j in range(PACK - 1):
            for h in range(2):
                gather(v_pairs[h], v_planes[j], j, h * HALF, (h + 1) * HALF)
        for h in range(2):
            gather(v_pairs[h], v_planes[PACK - 1], PACK - 1, h * HALF, (h + 1) * HALF)
        for h in range(2):
            group_pairs(vcopy, v_op, h * HALF, v_pairs[h], 0, HALF)
        for h in range(2):
            quantize(v_op, h * HALF, (h + 1) * HALF)
        group_sorted(vcopy, do_op, do_raw, 0, 2)
        group_sorted(scopy, do_op, do_raw, 2, 2)
        quantize(do_op, 0, HALF)
        quantize(do_op, HALF, W)

        dp_banks = [psum.tile([P, 2, HALF], F32, name="dp%d" % i, tag="first%d" % i) for i in range(PACK)]
        for h in range(2):
            for t in range(PACK):
                matmul(dp_banks[2 * h + t // 2][:, t % 2, :], do_op, t * P, v_op, h * HALF, (h + 1) * HALF)
        for h in range(2):
            for t in range(PACK):
                nc.vector.scalar_tensor_tensor(
                    ds_rows[h][:, t, :],
                    dp_banks[2 * h + t // 2][:, t % 2, :],
                    gate2[:, t : t + 1],
                    relu_a[2 * h + t // 2][:, t % 2, :],
                    MULT,
                    MULT,
                )
        group(scopy, ds_op, 0, ds_rows[0], 0, HALF)
        group(vcopy, ds_op, HALF, ds_rows[1], 0, HALF)

        for n in range(PACK):
            output_tile(n, (dom_ops[n], 0), pw_op, True, "second%d" % n, dense_tile("dense%d" % n, W, "do_raw" if n == PACK - 1 else "dense%d" % (n % 2))[:])

        group(vcopy, qm_first, 0, qm_raw, 0, P)
        quantize(qm_first, 0, P)
        quantize(ds_op, 0, HALF)
        quantize(ds_op, HALF, W)
        for h in range(2):
            dense = dense_tile("dense4_%d" % h, HALF, "dense%d" % h)[:]
            product(4, (qm_first, 0), ds_op, h * HALF, (h + 1) * HALF, "second%d" % h, dense)
            scatter(4, dense, h * HALF, (h + 1) * HALF, False)
        store(4)
        qm_second = operand("qm_second", E4M3, P, "ds_rows0")
        group(scopy, qm_second, 0, qm_raw, P, P)
        quantize(qm_second, 0, P)
        qm_rest = operand("qm_rest", E4M3, HALF, "dense0")
        group(scopy, qm_rest, 0, qm_raw, HALF, HALF)
        quantize(qm_rest, 0, HALF)
        output_tile(5, (qm_second, 0), ds_op, False, "second2", dense_tile("dense5", W, "dense2")[:])
        output_tile(6, (qm_rest, 0), ds_op, False, "second3", dense_tile("dense6", W, "dense3")[:])
        output_tile(7, (qm_rest, P), ds_op, False, "second0", dense_tile("dense7", W, "dense0")[:])
